import numpy as np
import ml_dtypes


def mxq(x, axis, fmt="e4m3"):
    dtype, down = {"e4m3": (ml_dtypes.float8_e4m3fn, 7), "e5m2": (ml_dtypes.float8_e5m2, 14)}[fmt]
    v = np.moveaxis(np.asarray(x, np.float32).astype(ml_dtypes.bfloat16).astype(np.float64), axis, -1)
    blocks = v.reshape(v.shape[:-1] + (-1, 32))
    amax = np.abs(blocks).max(-1, keepdims=True)
    byte = np.maximum(np.where(amax > 0, np.frexp(amax)[1] - 1 + 127, 0) - down, 1)
    scale = np.exp2(byte - 127.0)
    codes = (blocks / scale).astype(np.float32).astype(dtype).astype(np.float64)
    return np.moveaxis((codes * scale).reshape(v.shape), -1, axis)


WIDE = False


def mx_kscale(k):
    if not WIDE:
        return np.ones(k)
    levels = np.array([10, -10, 5, -5, 0])
    if k % 512:
        return np.exp2(np.random.permutation(np.resize(levels, k // 32))).repeat(32)
    a = np.empty((k // 512, 16))
    for p in range(k // 512):
        a[p, :8] = np.random.permutation(np.resize(levels, 8))
        for g in range(8):
            far = levels[np.abs(levels - a[p, g]) >= 10]
            a[p, g + 8] = far[np.random.randint(len(far))]
    return np.exp2(a.ravel()).repeat(32)


def f64(x):
    return np.asarray(x).astype(np.float64)


def striped(idx):
    return np.tile(idx.reshape(-1, 16).T, (8, 1)).astype(np.uint16)


def unstriped(offs):
    return offs[:16].T.reshape(-1).astype(np.int64)


E2M1 = np.array([0.0, 0.5, 1.0, 1.5, 2.0, 3.0, 4.0, 6.0, -0.0, -0.5, -1.0, -1.5, -2.0, -3.0, -4.0, -6.0])


def pack_weight(w, fmt):
    k, n = w.shape
    w = f64(np.asarray(w, np.float32).astype(ml_dtypes.bfloat16)).reshape(k // 32, 32, n)
    amax = np.abs(w).max(1)
    if fmt == "e4m3":
        byte = np.frexp(amax)[1] - 1 + 127 - 7
    else:
        mant, ex = np.frexp(amax / 6.0)
        byte = np.where(mant > 0.5, ex, ex - 1) + 127
    byte = np.clip(np.where(amax > 0, byte, 1), 1, 254)
    scaled = (w * np.exp2(127.0 - byte)[:, None, :]).reshape(k, n).astype(np.float32)
    by_word = np.ascontiguousarray(scaled.reshape(k // 512, 128, 4, n).transpose(0, 1, 3, 2))
    if fmt == "e4m3":
        words = by_word.astype(ml_dtypes.float8_e4m3fn).view(np.uint8)
    else:
        c = by_word.astype(ml_dtypes.float4_e2m1fn).view(np.uint8) & 0xF
        words = (c[..., 0::2] | (c[..., 1::2] << 4)).reshape(k // 512, 128, 2 * n)
    return np.ascontiguousarray(words), np.ascontiguousarray(byte.astype(np.uint8).reshape(k // 512, 16, n))


def unpack_weight(words, scales, fmt):
    g, _, n = scales.shape
    words = np.ascontiguousarray(words).reshape(g, 128, n, -1)
    if fmt == "e4m3":
        vals = words.view(ml_dtypes.float8_e4m3fn).astype(np.float64)
    else:
        nib = np.empty((g, 128, n, 4), np.uint8)
        nib[..., 0::2] = words & 0xF
        nib[..., 1::2] = words >> 4
        vals = E2M1[nib]
    vals = vals * np.repeat(np.exp2(scales.astype(np.float64) - 127.0), 8, axis=1)[..., None]
    return vals.transpose(0, 1, 3, 2).reshape(g * 512, n)


def gelu(v):
    return 0.5 * v * (1.0 + np.tanh(np.sqrt(2.0 / np.pi) * (v + 0.044715 * v**3)))


T, S, T2, P, T3, S2, K, K2, H = 2048, 1024, 2048, 1024, 2048, 512, 1024, 512, 1024

def setup_inputs():
    n = np.random.standard_normal
    s = mx_kscale(K)[:, None]
    s2 = mx_kscale(K2)[:, None]
    u = mx_kscale(H)[:, None]
    tab_words, tab_scales = pack_weight(n((K, T)) * s, "e4m3")
    tab2_words, tab2_scales = pack_weight(n((H, T3)) / np.sqrt(H) / u, "e4m3")
    w4_words, w4_scales = pack_weight(n((K, H)) / np.sqrt(K) / s, "e2m1")
    return {
        "tab_words": tab_words, "tab_scales": tab_scales,
        "offs": striped(np.random.permutation(T)[:S]),
        "w4_words": w4_words, "w4_scales": w4_scales,
        "hand": (n((K2, S)) * s2).astype(np.float32),
        "wh": (n((K2, H)) / np.sqrt(K2) / s2).astype(np.float32),
        "gain": (np.exp(0.3 * n(H)) * u[:, 0]).astype(np.float32),
        "page0": (n((H, T2)) * u).astype(np.float32),
        "wgs": np.exp(0.3 * n((128, S))).astype(np.float32),
        "offs3": striped(np.random.permutation(T2)[:S]),
        "tab2_words": tab2_words, "tab2_scales": tab2_scales,
        "offs2": striped(np.random.permutation(T3)[:S2]),
        "offs4": striped(np.random.permutation(T2)[:P]),
        "cap": (0.5 + 0.7 * n((S2, P))).astype(np.float32),
    }

def reference(tab_words, tab_scales, offs, w4_words, w4_scales, hand, wh, gain, page0, wgs, offs3,
              tab2_words, tab2_scales, offs2, offs4, cap):
    v = unpack_weight(tab_words, tab_scales, "e4m3")[:, unstriped(offs)]
    v2 = unpack_weight(tab2_words, tab2_scales, "e4m3")[:, unstriped(offs2)]
    w4 = unpack_weight(w4_words, w4_scales, "e2m1")
    x = w4.T @ v + mxq(f64(wh), 0, "e4m3").T @ mxq(f64(hand), 0, "e4m3")
    gelu = 0.5 * x * (1.0 + np.tanh(0.7978845608028654 * (x + 0.044715 * x * x * x)))
    h = f64(gain)[:, None] * gelu
    page = f64(page0).copy()
    page[:, unstriped(offs3)] = np.tile(f64(wgs), (H // 128, 1)) * h
    e = v2.T @ mxq(page, 0, "e4m3")
    return np.minimum(e[:, unstriped(offs4)], f64(cap))

@@ -1,0 +1,285 @@
+from contextlib import ExitStack
+
+import concourse.mybir as mybir
+
+F32 = mybir.dt.float32
+BF16 = mybir.dt.bfloat16
+I32 = mybir.dt.int32
+U32 = mybir.dt.uint32
+U16 = mybir.dt.uint16
+U8 = mybir.dt.uint8
+FP8X4 = mybir.dt.float8_e4m3fn_x4
+FP4X4 = mybir.dt.float4_e2m1fn_x4
+MULT = mybir.AluOpType.mult
+MIN = mybir.AluOpType.min
+GELU = mybir.ActivationFunctionType.Gelu_apprx_tanh
+COPY = mybir.ActivationFunctionType.Copy
+
+P = 128
+T = 2048
+S = 1024
+S2 = 512
+H = 1024
+N = 512
+FLOPS = 5368709120
+
+
+def tile_list_drop_move_adviser_kernel(
+    tc, tab_words, tab_scales, offs, w4_words, w4_scales, hand, wh, gain, page0, wgs, offs3,
+    tab2_words, tab2_scales, offs2, offs4, cap, out,
+):
+    nc = tc.nc
+    with ExitStack() as ctx:
+        held = ctx.enter_context(tc.tile_pool(name="held", bufs=1))
+        ring = ctx.enter_context(tc.tile_pool(name="ring", bufs=1))
+        psum = ctx.enter_context(tc.psum_pool(name="psum", bufs=1))
+        banks = [psum.tile([P, N], F32, name=f"bank{b}") for b in range(8)]
+
+        def keep(shape, dtype, name):
+            return held.tile(shape, dtype, name=name, align_bytes=64)
+
+        def rotating(shape, dtype, tag, bufs, name):
+            return ring.tile(shape, dtype, name=name, tag=tag, bufs=bufs, align_bytes=64)
+
+        def load_list(src, name):
+            lst = held.tile(list(src.shape), U16, name=name)
+            nc.sync.dma_start(lst[:], src)
+            return lst
+
+        def load_table_scales(queue, src, name):
+            plane = keep([P, T], U8, name)
+            nc.vector.memset(plane[:].bitcast(I32), 0)
+            for q in range(4):
+                queue.dma_start(plane[32 * q : 32 * q + 8, :].bitcast(I32), src[:, 4 * q : 4 * q + 4, :].bitcast(I32))
+            return plane
+
+        def load_table_words(src, a, name):
+            words = rotating([P, T], U32, "table", 2, name)
+            nc.sync.dma_start(words[:].bitcast(I32), src[a].rearrange("p t i -> p (t i)").bitcast(I32))
+            return words
+
+        def load_rows(src, b, name):
+            raw = rotating([P, 4, N], F32, "raw", 3, name)
+            nc.sync.dma_start(raw[:], src[:, b * N : (b + 1) * N].rearrange("(p j) c -> p j c", j=4))
+            return raw
+
+        def load_wgs(t0, t1):
+            rows = keep([P, t1 - t0, S], F32, f"wgs{t0}")
+            for q in range(4):
+                nc.sync.dma_start(rows[32 * q : 32 * q + 32, :, :], wgs.rearrange("(q t) j -> q t j", t=4)[:, t0:t1, :])
+            return [rows[:, t, :] for t in range(t1 - t0)]
+
+        def load_page(i):
+            a, t = divmod(i, 4)
+            tile = rotating([P, T], F32, "page", 5, f"page{i}")
+            nc.sync.dma_start(tile[:], page0.rearrange("(a p t) c -> a t p c", a=2, t=4)[a, t])
+            return tile
+
+        def quantize(grouped, name, codes=None):
+            if codes is None:
+                codes = keep([P, N], U32, name + "_codes")
+            scales = keep([P, N], U8, name + "_scales")
+            nc.vector.quantize_mx(out=codes[:].bitcast(FP8X4), scales=scales[:], in_=grouped[:])
+            return codes, scales
+
+        def group_wh(raw, grouped):
+            nc.scalar.activation(
+                grouped[:].rearrange("p (t m j) -> p m j t", t=4, j=4),
+                raw[:].rearrange("p j (m t) -> p m j t", t=4),
+                COPY,
+            )
+            return grouped
+
+        def group_hand(raw, name):
+            grouped = rotating([P, 4 * N], BF16, "grouped", 4, name)
+            nc.scalar.copy(
+                grouped[:].rearrange("p (c i j) -> p c j i", i=4, j=4),
+                raw[:].rearrange("p j (c i) -> p c j i", i=4),
+            )
+            return grouped
+
+        def load_planes_side_by_side(src, name):
+            planes = keep([P, 2, src.shape[2]], U8, name)
+            nc.vector.memset(planes[:].bitcast(I32), 0)
+            for q in range(4):
+                nc.sync.dma_start(
+                    planes[32 * q : 32 * q + 4, :, :].bitcast(I32),
+                    src[:, 4 * q : 4 * q + 4, :].rearrange("k r n -> r k n").bitcast(I32),
+                )
+            return planes
+
+        idx = load_list(offs, "idx")
+        idx2 = load_list(offs2, "idx2")
+        idx3 = load_list(offs3, "idx3")
+        idx4 = load_list(offs4, "idx4")
+        gains = keep([P, 2, 4], F32, "gains")
+        nc.sync.dma_start(gains[:], gain.rearrange("(a p t) -> p a t", a=2, t=4))
+        w4_raw = keep([P, 2, 512], I32, "w4_raw")
+        for k in range(2):
+            nc.sync.dma_start(w4_raw[:, k, :], w4_words[k].bitcast(I32))
+        wh_raw = [load_rows(wh, 0, "wh_raw0")]
+        tab_plane = load_table_scales(nc.sync, tab_scales, "tab_plane")
+        hand_raw = [load_rows(hand, 0, "hand_raw0")]
+        w4_plane_raw = load_planes_side_by_side(w4_scales, "w4_plane_raw")
+        tab = [load_table_words(tab_words, 0, "tab0")]
+        hand_raw.append(load_rows(hand, 1, "hand_raw1"))
+        tab.append(load_table_words(tab_words, 1, "tab1"))
+        pages = [load_page(0)]
+        wgs_rows = load_wgs(0, 1)
+
+        def gather_v(k, h):
+            words = keep([P, N], U32, f"v{k}{h}")
+            nc.vector.tensor_copy(words[:], tab[k][:].indirect(idx[:, 32 * h : 32 * h + 32]))
+            return words
+
+        w4 = keep([P, 2, 2 * H], U8, "w4")
+        nc.vector.tensor_copy(
+            w4[:].bitcast(U16).rearrange("p k (a t m) -> p (k a) t m", a=2, t=4),
+            w4_raw[:].bitcast(U16).rearrange("p k (a m t) -> p (k a) t m", a=2, t=4),
+        )
+        v_plane = [keep([P, S], U8, f"v_plane{k}") for k in range(2)]
+        nc.vector.memset(v_plane[1][:].bitcast(I32), 0)
+        nc.vector.tensor_copy(v_plane[0][:], tab_plane[:].indirect(idx[:]))
+        nc.scalar.dma_start(v_plane[1][0:100, :].bitcast(I32), v_plane[0][4:104, :].bitcast(I32))
+        w4_plane = keep([P, 2, H], U8, "w4_plane")
+        nc.vector.tensor_copy(
+            w4_plane[:].rearrange("p k (a t m) -> p (k a) t m", a=2, t=4),
+            w4_plane_raw[:].rearrange("p k (a m t) -> p (k a) t m", a=2, t=4),
+        )
+
+        whq = [quantize(group_wh(wh_raw[0], rotating([P, 4 * N], BF16, "grouped", 4, "wh_g0")), "wh0")]
+        v = [[gather_v(0, h) for h in range(2)]]
+        handq = [quantize(group_hand(hand_raw[0], "hand_g0"), "hand0")]
+        v.append([gather_v(1, h) for h in range(2)])
+        handq.append(quantize(group_hand(hand_raw[1], "hand_g1"), "hand1"))
+
+        wgs_rows = wgs_rows + load_wgs(1, 2)
+        pages.append(load_page(1))
+        wh_raw.append(load_rows(wh, 1, "wh_raw1"))
+        tab2_plane = load_table_scales(nc.sync, tab2_scales, "tab2_plane")
+        wgs_rows = wgs_rows + load_wgs(2, 4)
+        pages.append(load_page(2))
+        pages.append(load_page(3))
+        tab2 = [load_table_words(tab2_words, a, f"tab2_{a}") for a in range(2)]
+        pages.append(load_page(4))
+        caps = []
+        for u in range(2):
+            both = rotating([P, 2, S], F32, "raw", 3, f"cap{u}")
+            nc.sync.dma_start(both[:], cap.rearrange("(u w p) m -> u p w m", u=2, w=2)[u])
+            caps = caps + [both[:, 0, :], both[:, 1, :]]
+
+        def first_product(i):
+            a, t = divmod(i, 4)
+            act = rotating([P, S], F32, f"act{0 if i in (4, 7) else i}", 1, f"act{i}")
+            col = N * a + P * t
+            for h in range(2):
+                bank = banks[h]
+                cols = slice(h * N, (h + 1) * N)
+                passes = [(whq[a][0][:, P * t : P * (t + 1)].bitcast(FP8X4), whq[a][1][:, P * t : P * (t + 1)], handq[h][0], handq[h][1][:])]
+                for k in range(2):
+                    passes.append((w4[:, k, 2 * col : 2 * (col + P)].bitcast(FP4X4), w4_plane[:, k, col : col + P], v[k][h], v_plane[k][:, cols]))
+                if h == 1:
+                    passes = passes[::-1]
+                for step, (lhsT, lhsT_scale, rhs, rhs_scale) in enumerate(passes):
+                    nc.tensor.matmul_mx(
+                        out=bank[:], lhsT=lhsT, lhsT_scale=lhsT_scale, rhs=rhs[:].bitcast(FP8X4), rhs_scale=rhs_scale,
+                        start=(step == 0), stop=(step == 2),
+                    )
+                nc.scalar.activation(act[:, cols], bank[:], GELU)
+                nc.scalar.activation(act[:, cols], act[:, cols], COPY, scale=gains[:, a, t : t + 1])
+            return act
+
+        def scatter(i, act, pieces):
+            width = S // pieces
+            for h in range(pieces):
+                cols = slice(h * width, (h + 1) * width)
+                nc.vector.tensor_tensor(
+                    pages[i][:].indirect(idx3[:, h * width // 16 : (h + 1) * width // 16]), act[:, cols], wgs_rows[i % 4][:, cols], MULT
+                )
+
+        def round_into_pairs(i, c, pairs):
+            t = i % 4
+            nc.scalar.copy(pairs[:, t // 2, :, t % 2], pages[i][:, c * N : (c + 1) * N])
+
+        def weave(copy, pairs, name, tag="grouped", bufs=4):
+            grouped = rotating([P, 4 * N], BF16, tag, bufs, name)
+            copy(
+                grouped[:].bitcast(F32).rearrange("p (c i u) -> p c u i", i=4, u=2),
+                pairs[:].rearrange("p u c e -> p u (c e)").bitcast(F32).rearrange("p u (c i) -> p c u i", i=4),
+            )
+            return grouped
+
+        def gather_v2(u, tag):
+            words = rotating([P, 2, S2 // 2], U32, tag, 1, f"v2_{u}")
+            for b in range(2):
+                nc.vector.tensor_copy(words[:, b, :], tab2[b][:].indirect(idx2[:, 16 * u : 16 * u + 16]))
+            return words
+
+        def second_product(n, c, a):
+            rows = slice(P * n, P * (n + 1))
+            nc.tensor.matmul_mx(
+                out=banks[4 * ((n + 1) % 2) + c][:], lhsT=v2[n // 2][:, a, P * (n % 2) : P * (n % 2 + 1)].bitcast(FP8X4), lhsT_scale=v2_plane[4 * a : P, rows],
+                rhs=pageq[a][c][0][:].bitcast(FP8X4), rhs_scale=pageq[a][c][1][:], start=(a == 0), stop=(a == 1),
+            )
+
+        ahead = [first_product(i) for i in range(4)]
+        pageq = [[], []]
+        for i in range(8):
+            a, t = divmod(i, 4)
+            scatter(i, ahead[i], 2 if i == 0 else 1)
+            if i == 0:
+                wh_g1 = group_wh(wh_raw[1], rotating([P, 4 * N], BF16, "act0", 1, "wh_g1"))
+            if i == 1:
+                v2_plane = rotating([P, S2], U8, "act1", 1, "v2_plane")
+                nc.vector.tensor_copy(v2_plane[:], tab2_plane[:].indirect(idx2[:]))
+            if i == 2:
+                whq.append(quantize(wh_g1, "wh1", rotating([P, N], U32, "act2", 1, "wh1_codes")))
+            if i == 3:
+                v2 = [gather_v2(0, "act3")]
+            if t == 0:
+                pairs = [rotating([P, 2, N, 2], BF16, "pairs", 4, f"pairs{a}{c}") for c in range(4)]
+            if i < 7:
+                for c in range(4):
+                    round_into_pairs(i, c, pairs[c])
+            if i + 5 < 8:
+                pages.append(load_page(i + 5))
+            if i == 2:
+                ahead.extend([first_product(4), first_product(5)])
+            if i in (3, 4):
+                ahead.append(first_product(i + 3))
+            if i == 3:
+                woven = [weave(nc.scalar.copy, pairs[c], f"page_g0{c}") for c in range(4)]
+            if i in (5, 6):
+                both = rotating([P, 2, N], U32, f"act{i}", 1, f"page0_codes{i}")
+                for u in range(2):
+                    c = 2 * (i - 5) + u
+                    pageq[0].append(quantize(woven[c], f"page0{c}", both[:, u, :]))
+        for n in range(2):
+            for c in range(4):
+                second_product(n, c, 0)
+
+        scores = [rotating([P, T], F32, "page", 5, f"scores{n}") for n in range(4)]
+        for c in range(4):
+            round_into_pairs(7, c, pairs[c])
+        for c in range(4):
+            if c < 3:
+                grouped = weave(nc.vector.tensor_copy, pairs[c], f"page_g1{c}")
+            else:
+                grouped = weave(nc.vector.tensor_copy, pairs[c], f"page_g1{c}", "act0", 1)
+            pageq[1].append(quantize(grouped, f"page1{c}"))
+            for n in range(2):
+                second_product(n, c, 1)
+        v2.append(gather_v2(1, "act0"))
+        for n in range(4):
+            for c in range(4):
+                if n >= 2:
+                    for a in range(2):
+                        second_product(n, c, a)
+                nc.scalar.copy(scores[n][:, c * N : (c + 1) * N], banks[4 * ((n + 1) % 2) + c][:])
+            edges = [0, 512, 768, S] if n == 3 else [0, S]
+            for lo, hi in zip(edges[:-1], edges[1:]):
+                cols = slice(lo, hi)
+                picked = rotating([P, hi - lo], F32, "picked", 4, f"picked{n}_{lo}")
+                nc.vector.tensor_copy(picked[:], scores[n][:].indirect(idx4[:, lo // 16 : hi // 16]))
+                nc.vector.tensor_tensor(picked[:], picked[:], caps[n][:, cols], MIN)
+                nc.sync.dma_start(out[P * n : P * (n + 1), cols], picked[:])

@@ -109,20 +109,19 @@ def tile_list_drop_move_adviser_kernel(
             return planes
 
         idx = load_list(offs, "idx")
-        idx2 = load_list(offs2, "idx2")
-        idx3 = load_list(offs3, "idx3")
-        idx4 = load_list(offs4, "idx4")
         gains = keep([P, 2, 4], F32, "gains")
         nc.sync.dma_start(gains[:], gain.rearrange("(a p t) -> p a t", a=2, t=4))
+        idx3 = load_list(offs3, "idx3")
+        idx2 = load_list(offs2, "idx2")
         w4_raw = keep([P, 2, 512], I32, "w4_raw")
-        for k in range(2):
-            nc.sync.dma_start(w4_raw[:, k, :], w4_words[k].bitcast(I32))
+        nc.sync.dma_start(w4_raw[:], w4_words.rearrange("k p b -> p k b").bitcast(I32))
+        tab = [load_table_words(tab_words, 0, "tab0")]
         wh_raw = [load_rows(wh, 0, "wh_raw0")]
+        idx4 = load_list(offs4, "idx4")
         tab_plane = load_table_scales(nc.sync, tab_scales, "tab_plane")
         hand_raw = [load_rows(hand, 0, "hand_raw0")]
-        w4_plane_raw = load_planes_side_by_side(w4_scales, "w4_plane_raw")
-        tab = [load_table_words(tab_words, 0, "tab0")]
         hand_raw.append(load_rows(hand, 1, "hand_raw1"))
+        w4_plane_raw = load_planes_side_by_side(w4_scales, "w4_plane_raw")
         tab.append(load_table_words(tab_words, 1, "tab1"))
         pages = [load_page(0)]
         wgs_rows = load_wgs(0, 1)
@@ -137,10 +136,11 @@ def tile_list_drop_move_adviser_kernel(
             w4[:].bitcast(U16).rearrange("p k (a t m) -> p (k a) t m", a=2, t=4),
             w4_raw[:].bitcast(U16).rearrange("p k (a m t) -> p (k a) t m", a=2, t=4),
         )
+        v = [[gather_v(0, h) for h in range(2)]]
         v_plane = [keep([P, S], U8, f"v_plane{k}") for k in range(2)]
         nc.vector.memset(v_plane[1][:].bitcast(I32), 0)
         nc.vector.tensor_copy(v_plane[0][:], tab_plane[:].indirect(idx[:]))
-        nc.scalar.dma_start(v_plane[1][0:100, :].bitcast(I32), v_plane[0][4:104, :].bitcast(I32))
+        nc.gpsimd.dma_start(v_plane[1][0:100, :].bitcast(I32), v_plane[0][4:104, :].bitcast(I32))
         w4_plane = keep([P, 2, H], U8, "w4_plane")
         nc.vector.tensor_copy(
             w4_plane[:].rearrange("p k (a t m) -> p (k a) t m", a=2, t=4),
@@ -148,17 +148,16 @@ def tile_list_drop_move_adviser_kernel(
         )
 
         whq = [quantize(group_wh(wh_raw[0], rotating([P, 4 * N], BF16, "grouped", 4, "wh_g0")), "wh0")]
-        v = [[gather_v(0, h) for h in range(2)]]
         handq = [quantize(group_hand(hand_raw[0], "hand_g0"), "hand0")]
         v.append([gather_v(1, h) for h in range(2)])
         handq.append(quantize(group_hand(hand_raw[1], "hand_g1"), "hand1"))
 
-        wgs_rows = wgs_rows + load_wgs(1, 2)
-        pages.append(load_page(1))
         wh_raw.append(load_rows(wh, 1, "wh_raw1"))
-        tab2_plane = load_table_scales(nc.sync, tab2_scales, "tab2_plane")
-        wgs_rows = wgs_rows + load_wgs(2, 4)
+        pages.append(load_page(1))
+        wgs_rows = wgs_rows + load_wgs(1, 2)
         pages.append(load_page(2))
+        wgs_rows = wgs_rows + load_wgs(2, 4)
+        tab2_plane = load_table_scales(nc.sync, tab2_scales, "tab2_plane")
         pages.append(load_page(3))
         tab2 = [load_table_words(tab2_words, a, f"tab2_{a}") for a in range(2)]
         pages.append(load_page(4))
@@ -186,7 +185,10 @@ def tile_list_drop_move_adviser_kernel(
                         start=(step == 0), stop=(step == 2),
                     )
                 nc.scalar.activation(act[:, cols], bank[:], GELU)
-                nc.scalar.activation(act[:, cols], act[:, cols], COPY, scale=gains[:, a, t : t + 1])
+                if i == 0:
+                    nc.scalar.activation(act[:, cols], act[:, cols], COPY, scale=gains[:, a, t : t + 1])
+            if i > 0:
+                nc.scalar.activation(act[:], act[:], COPY, scale=gains[:, a, t : t + 1])
             return act
 
         def scatter(i, act, pieces):
@@ -199,13 +201,13 @@ def tile_list_drop_move_adviser_kernel(
 
         def round_into_pairs(i, c, pairs):
             t = i % 4
-            nc.scalar.copy(pairs[:, t // 2, :, t % 2], pages[i][:, c * N : (c + 1) * N])
+            nc.scalar.copy(pairs[:, t, :], pages[i][:, c * N : (c + 1) * N])
 
         def weave(copy, pairs, name, tag="grouped", bufs=4):
             grouped = rotating([P, 4 * N], BF16, tag, bufs, name)
             copy(
-                grouped[:].bitcast(F32).rearrange("p (c i u) -> p c u i", i=4, u=2),
-                pairs[:].rearrange("p u c e -> p u (c e)").bitcast(F32).rearrange("p u (c i) -> p c u i", i=4),
+                grouped[:].rearrange("p (c i t) -> p c t i", i=4, t=4),
+                pairs[:].rearrange("p t (c i) -> p c t i", i=4),
             )
             return grouped
 
@@ -230,23 +232,23 @@ def tile_list_drop_move_adviser_kernel(
             if i == 0:
                 wh_g1 = group_wh(wh_raw[1], rotating([P, 4 * N], BF16, "act0", 1, "wh_g1"))
             if i == 1:
-                v2_plane = rotating([P, S2], U8, "act1", 1, "v2_plane")
-                nc.vector.tensor_copy(v2_plane[:], tab2_plane[:].indirect(idx2[:]))
+                whq.append(quantize(wh_g1, "wh1", rotating([P, N], U32, "act1", 1, "wh1_codes")))
             if i == 2:
-                whq.append(quantize(wh_g1, "wh1", rotating([P, N], U32, "act2", 1, "wh1_codes")))
+                v2_plane = rotating([P, S2], U8, "act2", 1, "v2_plane")
+                nc.vector.tensor_copy(v2_plane[:], tab2_plane[:].indirect(idx2[:]))
             if i == 3:
                 v2 = [gather_v2(0, "act3")]
             if t == 0:
-                pairs = [rotating([P, 2, N, 2], BF16, "pairs", 4, f"pairs{a}{c}") for c in range(4)]
+                pairs = [rotating([P, 4, N], BF16, "pairs", 4, f"pairs{a}{c}") for c in range(4)]
             if i < 7:
                 for c in range(4):
                     round_into_pairs(i, c, pairs[c])
             if i + 5 < 8:
                 pages.append(load_page(i + 5))
-            if i == 2:
+            if i == 1:
                 ahead.extend([first_product(4), first_product(5)])
-            if i in (3, 4):
-                ahead.append(first_product(i + 3))
+            if i in (2, 4):
+                ahead.append(first_product(len(ahead)))
             if i == 3:
                 woven = [weave(nc.scalar.copy, pairs[c], f"page_g0{c}") for c in range(4)]
             if i in (5, 6):
@@ -265,7 +267,7 @@ def tile_list_drop_move_adviser_kernel(
             if c < 3:
                 grouped = weave(nc.vector.tensor_copy, pairs[c], f"page_g1{c}")
             else:
-                grouped = weave(nc.vector.tensor_copy, pairs[c], f"page_g1{c}", "act0", 1)
+                grouped = weave(nc.scalar.copy, pairs[c], f"page_g1{c}", "act0", 1)
             pageq[1].append(quantize(grouped, f"page1{c}"))
             for n in range(2):
                 second_product(n, c, 1)

@@ -64,8 +64,8 @@ def tile_list_drop_move_adviser_kernel(
             return raw
 
         def load_wgs(t0, t1):
-            rows = keep([P, t1 - t0, S], F32, f"wgs{t0}")
-            for q in range(4):
+            rows = rotating([P, t1 - t0, S], F32, f"wgs{t0}", 1, f"wgs{t0}")
+            for q in (0, 2, 1, 3):
                 nc.sync.dma_start(rows[32 * q : 32 * q + 32, :, :], wgs.rearrange("(q t) j -> q t j", t=4)[:, t0:t1, :])
             return [rows[:, t, :] for t in range(t1 - t0)]
 
@@ -102,45 +102,43 @@ def tile_list_drop_move_adviser_kernel(
             planes = keep([P, 2, src.shape[2]], U8, name)
             nc.vector.memset(planes[:].bitcast(I32), 0)
             for q in range(4):
-                nc.sync.dma_start(
+                nc.gpsimd.dma_start(
                     planes[32 * q : 32 * q + 4, :, :].bitcast(I32),
                     src[:, 4 * q : 4 * q + 4, :].rearrange("k r n -> r k n").bitcast(I32),
                 )
             return planes
 
+        tab_plane = load_table_scales(nc.gpsimd, tab_scales, "tab_plane")
+        w4_plane_raw = load_planes_side_by_side(w4_scales, "w4_plane_raw")
         idx = load_list(offs, "idx")
         gains = keep([P, 2, 4], F32, "gains")
         nc.sync.dma_start(gains[:], gain.rearrange("(a p t) -> p a t", a=2, t=4))
-        idx3 = load_list(offs3, "idx3")
-        idx2 = load_list(offs2, "idx2")
         w4_raw = keep([P, 2, 512], I32, "w4_raw")
         nc.sync.dma_start(w4_raw[:], w4_words.rearrange("k p b -> p k b").bitcast(I32))
         tab = [load_table_words(tab_words, 0, "tab0")]
         wh_raw = [load_rows(wh, 0, "wh_raw0")]
-        idx4 = load_list(offs4, "idx4")
-        tab_plane = load_table_scales(nc.sync, tab_scales, "tab_plane")
-        hand_raw = [load_rows(hand, 0, "hand_raw0")]
-        hand_raw.append(load_rows(hand, 1, "hand_raw1"))
-        w4_plane_raw = load_planes_side_by_side(w4_scales, "w4_plane_raw")
+        hand_raw = [load_rows(hand, h, f"hand_raw{h}") for h in range(2)]
         tab.append(load_table_words(tab_words, 1, "tab1"))
         pages = [load_page(0)]
+        idx3 = load_list(offs3, "idx3")
         wgs_rows = load_wgs(0, 1)
 
-        def gather_v(k, h):
-            words = keep([P, N], U32, f"v{k}{h}")
-            nc.vector.tensor_copy(words[:], tab[k][:].indirect(idx[:, 32 * h : 32 * h + 32]))
-            return words
+        def gather_v(k):
+            words = rotating([P, 2, N], U32, f"v{k}", 1, f"v{k}")
+            for h in range(2):
+                nc.vector.tensor_copy(words[:, h, :], tab[k][:].indirect(idx[:, 32 * h : 32 * h + 32]))
+            return [words[:, h, :] for h in range(2)]
 
         w4 = keep([P, 2, 2 * H], U8, "w4")
         nc.vector.tensor_copy(
             w4[:].bitcast(U16).rearrange("p k (a t m) -> p (k a) t m", a=2, t=4),
             w4_raw[:].bitcast(U16).rearrange("p k (a m t) -> p (k a) t m", a=2, t=4),
         )
-        v = [[gather_v(0, h) for h in range(2)]]
         v_plane = [keep([P, S], U8, f"v_plane{k}") for k in range(2)]
         nc.vector.memset(v_plane[1][:].bitcast(I32), 0)
         nc.vector.tensor_copy(v_plane[0][:], tab_plane[:].indirect(idx[:]))
         nc.gpsimd.dma_start(v_plane[1][0:100, :].bitcast(I32), v_plane[0][4:104, :].bitcast(I32))
+        v = [gather_v(0)]
         w4_plane = keep([P, 2, H], U8, "w4_plane")
         nc.vector.tensor_copy(
             w4_plane[:].rearrange("p k (a t m) -> p (k a) t m", a=2, t=4),
@@ -149,7 +147,7 @@ def tile_list_drop_move_adviser_kernel(
 
         whq = [quantize(group_wh(wh_raw[0], rotating([P, 4 * N], BF16, "grouped", 4, "wh_g0")), "wh0")]
         handq = [quantize(group_hand(hand_raw[0], "hand_g0"), "hand0")]
-        v.append([gather_v(1, h) for h in range(2)])
+        v.append(gather_v(1))
         handq.append(quantize(group_hand(hand_raw[1], "hand_g1"), "hand1"))
 
         wh_raw.append(load_rows(wh, 1, "wh_raw1"))
@@ -157,15 +155,12 @@ def tile_list_drop_move_adviser_kernel(
         wgs_rows = wgs_rows + load_wgs(1, 2)
         pages.append(load_page(2))
         wgs_rows = wgs_rows + load_wgs(2, 4)
-        tab2_plane = load_table_scales(nc.sync, tab2_scales, "tab2_plane")
+        tab2_plane = load_table_scales(nc.gpsimd, tab2_scales, "tab2_plane")
+        idx2 = load_list(offs2, "idx2")
+        idx4 = load_list(offs4, "idx4")
         pages.append(load_page(3))
         tab2 = [load_table_words(tab2_words, a, f"tab2_{a}") for a in range(2)]
         pages.append(load_page(4))
-        caps = []
-        for u in range(2):
-            both = rotating([P, 2, S], F32, "raw", 3, f"cap{u}")
-            nc.sync.dma_start(both[:], cap.rearrange("(u w p) m -> u p w m", u=2, w=2)[u])
-            caps = caps + [both[:, 0, :], both[:, 1, :]]
 
         def first_product(i):
             a, t = divmod(i, 4)
@@ -256,6 +251,10 @@ def tile_list_drop_move_adviser_kernel(
                 for u in range(2):
                     c = 2 * (i - 5) + u
                     pageq[0].append(quantize(woven[c], f"page0{c}", both[:, u, :]))
+        caps = []
+        for n, tag in enumerate(("wgs0", "v0", "v1", "wgs1")):
+            caps.append(rotating([P, S], F32, tag, 1, f"cap{n}"))
+            nc.sync.dma_start(caps[n][:], cap[P * n : P * (n + 1), :])
         for n in range(2):
             for c in range(4):
                 second_product(n, c, 0)
@@ -263,15 +262,22 @@ def tile_list_drop_move_adviser_kernel(
         scores = [rotating([P, T], F32, "page", 5, f"scores{n}") for n in range(4)]
         for c in range(4):
             round_into_pairs(7, c, pairs[c])
+        woven = [weave(nc.vector.tensor_copy, pairs[0], "page_g10")]
         for c in range(4):
-            if c < 3:
-                grouped = weave(nc.vector.tensor_copy, pairs[c], f"page_g1{c}")
-            else:
-                grouped = weave(nc.scalar.copy, pairs[c], f"page_g1{c}", "act0", 1)
-            pageq[1].append(quantize(grouped, f"page1{c}"))
+            if c < 2:
+                woven.append(weave(nc.vector.tensor_copy, pairs[c + 1], f"page_g1{c + 1}"))
+            if c == 2:
+                woven.append(weave(nc.scalar.copy, pairs[3], "page_g13", "act0", 1))
+            pageq[1].append(quantize(woven[c], f"page1{c}"))
             for n in range(2):
                 second_product(n, c, 1)
         v2.append(gather_v2(1, "act0"))
+
+        def cap_and_store(n, cols, picked):
+            nc.vector.tensor_tensor(picked[:], picked[:], caps[n][:, cols], MIN)
+            nc.sync.dma_start(out[P * n : P * (n + 1), cols], picked[:])
+
+        waiting = []
         for n in range(4):
             for c in range(4):
                 if n >= 2:
@@ -280,8 +286,9 @@ def tile_list_drop_move_adviser_kernel(
                 nc.scalar.copy(scores[n][:, c * N : (c + 1) * N], banks[4 * ((n + 1) % 2) + c][:])
             edges = [0, 512, 768, S] if n == 3 else [0, S]
             for lo, hi in zip(edges[:-1], edges[1:]):
-                cols = slice(lo, hi)
                 picked = rotating([P, hi - lo], F32, "picked", 4, f"picked{n}_{lo}")
                 nc.vector.tensor_copy(picked[:], scores[n][:].indirect(idx4[:, lo // 16 : hi // 16]))
-                nc.vector.tensor_tensor(picked[:], picked[:], caps[n][:, cols], MIN)
-                nc.sync.dma_start(out[P * n : P * (n + 1), cols], picked[:])
+                waiting.append((n, slice(lo, hi), picked))
+                if len(waiting) == 2:
+                    cap_and_store(*waiting.pop(0))
+        cap_and_store(*waiting.pop(0))

@@ -63,11 +63,10 @@ def tile_list_drop_move_adviser_kernel(
             nc.sync.dma_start(raw[:], src[:, b * N : (b + 1) * N].rearrange("(p j) c -> p j c", j=4))
             return raw
 
-        def load_wgs(t0, t1):
-            rows = rotating([P, t1 - t0, S], F32, f"wgs{t0}", 1, f"wgs{t0}")
+        def load_wgs(rows, t0, cols):
+            planes = wgs.rearrange("(q t) j -> q t j", t=4)[:, t0 : t0 + rows.shape[1], cols]
             for q in (0, 2, 1, 3):
-                nc.sync.dma_start(rows[32 * q : 32 * q + 32, :, :], wgs.rearrange("(q t) j -> q t j", t=4)[:, t0:t1, :])
-            return [rows[:, t, :] for t in range(t1 - t0)]
+                nc.sync.dma_start(rows[32 * q : 32 * q + 32, :, cols], planes)
 
         def load_page(i):
             a, t = divmod(i, 4)
@@ -121,7 +120,9 @@ def tile_list_drop_move_adviser_kernel(
         tab.append(load_table_words(tab_words, 1, "tab1"))
         pages = [load_page(0)]
         idx3 = load_list(offs3, "idx3")
-        wgs_rows = load_wgs(0, 1)
+        wgs_tiles = [rotating([P, planes, S], F32, f"wgs{t0}", 1, f"wgs{t0}") for t0, planes in ((0, 1), (1, 1), (2, 2))]
+        wgs_rows = [wgs_tiles[0][:, 0, :], wgs_tiles[1][:, 0, :], wgs_tiles[2][:, 0, :], wgs_tiles[2][:, 1, :]]
+        load_wgs(wgs_tiles[0], 0, slice(0, N))
 
         def gather_v(k):
             words = rotating([P, 2, N], U32, f"v{k}", 1, f"v{k}")
@@ -150,11 +151,12 @@ def tile_list_drop_move_adviser_kernel(
         v.append(gather_v(1))
         handq.append(quantize(group_hand(hand_raw[1], "hand_g1"), "hand1"))
 
-        wh_raw.append(load_rows(wh, 1, "wh_raw1"))
         pages.append(load_page(1))
-        wgs_rows = wgs_rows + load_wgs(1, 2)
+        load_wgs(wgs_tiles[0], 0, slice(N, S))
+        wh_raw.append(load_rows(wh, 1, "wh_raw1"))
+        load_wgs(wgs_tiles[1], 1, slice(0, S))
         pages.append(load_page(2))
-        wgs_rows = wgs_rows + load_wgs(2, 4)
+        load_wgs(wgs_tiles[2], 2, slice(0, S))
         tab2_plane = load_table_scales(nc.gpsimd, tab2_scales, "tab2_plane")
         idx2 = load_list(offs2, "idx2")
         idx4 = load_list(offs4, "idx4")
@@ -196,13 +198,13 @@ def tile_list_drop_move_adviser_kernel(
 
         def round_into_pairs(i, c, pairs):
             t = i % 4
-            nc.scalar.copy(pairs[:, t, :], pages[i][:, c * N : (c + 1) * N])
+            nc.scalar.copy(pairs[:, t // 2, :, t % 2], pages[i][:, c * N : (c + 1) * N])
 
         def weave(copy, pairs, name, tag="grouped", bufs=4):
             grouped = rotating([P, 4 * N], BF16, tag, bufs, name)
             copy(
-                grouped[:].rearrange("p (c i t) -> p c t i", i=4, t=4),
-                pairs[:].rearrange("p t (c i) -> p c t i", i=4),
+                grouped[:].bitcast(F32).rearrange("p (c u) -> p c u", u=2),
+                pairs[:].rearrange("p u c e -> p u (c e)").bitcast(F32).rearrange("p u c -> p c u"),
             )
             return grouped
 
@@ -231,10 +233,8 @@ def tile_list_drop_move_adviser_kernel(
             if i == 2:
                 v2_plane = rotating([P, S2], U8, "act2", 1, "v2_plane")
                 nc.vector.tensor_copy(v2_plane[:], tab2_plane[:].indirect(idx2[:]))
-            if i == 3:
-                v2 = [gather_v2(0, "act3")]
             if t == 0:
-                pairs = [rotating([P, 4, N], BF16, "pairs", 4, f"pairs{a}{c}") for c in range(4)]
+                pairs = [rotating([P, 2, N, 2], BF16, "pairs", 4, f"pairs{a}{c}") for c in range(4)]
             if i < 7:
                 for c in range(4):
                     round_into_pairs(i, c, pairs[c])
@@ -246,32 +246,34 @@ def tile_list_drop_move_adviser_kernel(
                 ahead.append(first_product(len(ahead)))
             if i == 3:
                 woven = [weave(nc.scalar.copy, pairs[c], f"page_g0{c}") for c in range(4)]
-            if i in (5, 6):
-                both = rotating([P, 2, N], U32, f"act{i}", 1, f"page0_codes{i}")
-                for u in range(2):
-                    c = 2 * (i - 5) + u
-                    pageq[0].append(quantize(woven[c], f"page0{c}", both[:, u, :]))
         caps = []
         for n, tag in enumerate(("wgs0", "v0", "v1", "wgs1")):
             caps.append(rotating([P, S], F32, tag, 1, f"cap{n}"))
             nc.sync.dma_start(caps[n][:], cap[P * n : P * (n + 1), :])
-        for n in range(2):
-            for c in range(4):
-                second_product(n, c, 0)
 
         scores = [rotating([P, T], F32, "page", 5, f"scores{n}") for n in range(4)]
         for c in range(4):
             round_into_pairs(7, c, pairs[c])
-        woven = [weave(nc.vector.tensor_copy, pairs[0], "page_g10")]
-        for c in range(4):
-            if c < 2:
-                woven.append(weave(nc.vector.tensor_copy, pairs[c + 1], f"page_g1{c + 1}"))
-            if c == 2:
-                woven.append(weave(nc.scalar.copy, pairs[3], "page_g13", "act0", 1))
-            pageq[1].append(quantize(woven[c], f"page1{c}"))
+        v2 = [gather_v2(0, "act0")]
+        first_codes = rotating([P, 4, N], U32, "wgs2", 1, "page0_codes")
+
+        def quantize_and_multiply(a, c, grouped, codes=None):
+            pageq[a].append(quantize(grouped, f"page{a}{c}", codes))
             for n in range(2):
-                second_product(n, c, 1)
-        v2.append(gather_v2(1, "act0"))
+                second_product(n, c, a)
+
+        last = []
+        for c in range(2):
+            quantize_and_multiply(0, c, woven[c], first_codes[:, c, :])
+            last.append(weave(nc.vector.tensor_copy, pairs[c], f"page_g1{c}"))
+        for c in range(2, 4):
+            last.append(weave(nc.scalar.copy, pairs[c], f"page_g1{c}", f"act{c + 3}", 1))
+        for c in range(2):
+            quantize_and_multiply(1, c, last[c])
+            quantize_and_multiply(0, c + 2, woven[c + 2], first_codes[:, c + 2, :])
+        for c in range(2, 4):
+            quantize_and_multiply(1, c, last[c])
+        v2.append(gather_v2(1, "act6"))
 
         def cap_and_store(n, cols, picked):
             nc.vector.tensor_tensor(picked[:], picked[:], caps[n][:, cols], MIN)

@@ -32,6 +32,7 @@ def tile_list_drop_move_adviser_kernel(
     with ExitStack() as ctx:
         held = ctx.enter_context(tc.tile_pool(name="held", bufs=1))
         ring = ctx.enter_context(tc.tile_pool(name="ring", bufs=1))
+        placed = ctx.enter_context(tc.tile_pool(name="placed", bufs=1))
         psum = ctx.enter_context(tc.psum_pool(name="psum", bufs=1))
         banks = [psum.tile([P, N], F32, name=f"bank{b}") for b in range(8)]
 
@@ -47,7 +48,7 @@ def tile_list_drop_move_adviser_kernel(
             return lst
 
         def load_table_scales(queue, src, name):
-            plane = keep([P, T], U8, name)
+            plane = rotating([P, T], U8, name, 1, name)
             nc.vector.memset(plane[:].bitcast(I32), 0)
             for q in range(4):
                 queue.dma_start(plane[32 * q : 32 * q + 8, :].bitcast(I32), src[:, 4 * q : 4 * q + 4, :].bitcast(I32))
@@ -58,8 +59,8 @@ def tile_list_drop_move_adviser_kernel(
             nc.sync.dma_start(words[:].bitcast(I32), src[a].rearrange("p t i -> p (t i)").bitcast(I32))
             return words
 
-        def load_rows(src, b, name):
-            raw = rotating([P, 4, N], F32, "raw", 3, name)
+        def load_rows(src, b, place, name):
+            raw = placed.tile([P, 4, N], F32, name=name, offset=8192 * place, align_bytes=64)
             nc.sync.dma_start(raw[:], src[:, b * N : (b + 1) * N].rearrange("(p j) c -> p j c", j=4))
             return raw
 
@@ -98,7 +99,7 @@ def tile_list_drop_move_adviser_kernel(
             return grouped
 
         def load_planes_side_by_side(src, name):
-            planes = keep([P, 2, src.shape[2]], U8, name)
+            planes = rotating([P, 2, src.shape[2]], U8, name, 1, name)
             nc.vector.memset(planes[:].bitcast(I32), 0)
             for q in range(4):
                 nc.gpsimd.dma_start(
@@ -110,25 +111,27 @@ def tile_list_drop_move_adviser_kernel(
         tab_plane = load_table_scales(nc.gpsimd, tab_scales, "tab_plane")
         w4_plane_raw = load_planes_side_by_side(w4_scales, "w4_plane_raw")
         idx = load_list(offs, "idx")
-        gains = keep([P, 2, 4], F32, "gains")
-        nc.sync.dma_start(gains[:], gain.rearrange("(a p t) -> p a t", a=2, t=4))
         w4_raw = keep([P, 2, 512], I32, "w4_raw")
         nc.sync.dma_start(w4_raw[:], w4_words.rearrange("k p b -> p k b").bitcast(I32))
-        tab = [load_table_words(tab_words, 0, "tab0")]
-        wh_raw = [load_rows(wh, 0, "wh_raw0")]
-        hand_raw = [load_rows(hand, h, f"hand_raw{h}") for h in range(2)]
-        tab.append(load_table_words(tab_words, 1, "tab1"))
-        pages = [load_page(0)]
+        wh_raw = [load_rows(wh, 0, 0, "wh_raw0")]
+        hand_raw = [load_rows(hand, 0, 1, "hand_raw0")]
+        tab = [load_table_words(tab_words, k, f"tab{k}") for k in range(2)]
+        gains = keep([P, 2, 4], F32, "gains")
+        nc.sync.dma_start(gains[:], gain.rearrange("(a p t) -> p a t", a=2, t=4))
         idx3 = load_list(offs3, "idx3")
-        wgs_tiles = [rotating([P, planes, S], F32, f"wgs{t0}", 1, f"wgs{t0}") for t0, planes in ((0, 1), (1, 1), (2, 2))]
-        wgs_rows = [wgs_tiles[0][:, 0, :], wgs_tiles[1][:, 0, :], wgs_tiles[2][:, 0, :], wgs_tiles[2][:, 1, :]]
+        pages = [load_page(0)]
+        wgs_tiles = [rotating([P, 2, S], F32, f"wgs{t0}", 1, f"wgs{t0}") for t0 in (0, 2)]
+        wgs_rows = [wgs_tiles[t // 2][:, t % 2, :] for t in range(4)]
         load_wgs(wgs_tiles[0], 0, slice(0, N))
+        hand_raw.append(load_rows(hand, 1, 2, "hand_raw1"))
+        pages.append(load_page(1))
+        load_wgs(wgs_tiles[0], 0, slice(N, S))
 
-        def gather_v(k):
-            words = rotating([P, 2, N], U32, f"v{k}", 1, f"v{k}")
-            for h in range(2):
-                nc.vector.tensor_copy(words[:, h, :], tab[k][:].indirect(idx[:, 32 * h : 32 * h + 32]))
-            return [words[:, h, :] for h in range(2)]
+        v = [[None, None], [None, None]]
+
+        def gather_v(k, h, tag):
+            v[k][h] = rotating([P, N], U32, tag, 1, f"v{k}{h}")
+            nc.vector.tensor_copy(v[k][h][:], tab[k][:].indirect(idx[:, 32 * h : 32 * h + 32]))
 
         w4 = keep([P, 2, 2 * H], U8, "w4")
         nc.vector.tensor_copy(
@@ -139,80 +142,67 @@ def tile_list_drop_move_adviser_kernel(
         nc.vector.memset(v_plane[1][:].bitcast(I32), 0)
         nc.vector.tensor_copy(v_plane[0][:], tab_plane[:].indirect(idx[:]))
         nc.gpsimd.dma_start(v_plane[1][0:100, :].bitcast(I32), v_plane[0][4:104, :].bitcast(I32))
-        v = [gather_v(0)]
         w4_plane = keep([P, 2, H], U8, "w4_plane")
         nc.vector.tensor_copy(
             w4_plane[:].rearrange("p k (a t m) -> p (k a) t m", a=2, t=4),
             w4_plane_raw[:].rearrange("p k (a m t) -> p (k a) t m", a=2, t=4),
         )
-
         whq = [quantize(group_wh(wh_raw[0], rotating([P, 4 * N], BF16, "grouped", 4, "wh_g0")), "wh0")]
+        gather_v(0, 0, "tab_plane")
         handq = [quantize(group_hand(hand_raw[0], "hand_g0"), "hand0")]
-        v.append(gather_v(1))
-        handq.append(quantize(group_hand(hand_raw[1], "hand_g1"), "hand1"))
+        gather_v(1, 0, "w4_plane_raw")
+        gather_v(0, 1, "v01")
+        gather_v(1, 1, "v11")
 
-        pages.append(load_page(1))
-        load_wgs(wgs_tiles[0], 0, slice(N, S))
-        wh_raw.append(load_rows(wh, 1, "wh_raw1"))
-        load_wgs(wgs_tiles[1], 1, slice(0, S))
+        wh_raw.append(load_rows(wh, 1, 0, "wh_raw1"))
         pages.append(load_page(2))
-        load_wgs(wgs_tiles[2], 2, slice(0, S))
-        tab2_plane = load_table_scales(nc.gpsimd, tab2_scales, "tab2_plane")
+        load_wgs(wgs_tiles[1], 2, slice(0, S))
+        pages.append(load_page(3))
         idx2 = load_list(offs2, "idx2")
         idx4 = load_list(offs4, "idx4")
-        pages.append(load_page(3))
-        tab2 = [load_table_words(tab2_words, a, f"tab2_{a}") for a in range(2)]
+        tab2_plane = load_table_scales(nc.sync, tab2_scales, "tab2_plane")
         pages.append(load_page(4))
+        tab2 = [load_table_words(tab2_words, a, f"tab2_{a}") for a in range(2)]
 
-        def first_product(i):
+        act_tags = ["act0", "act1", "act2", "act3", "act0", "act1", "act6", "act7"]
+        acts = {}
+
+        def first_product(i, h):
             a, t = divmod(i, 4)
-            act = rotating([P, S], F32, f"act{0 if i in (4, 7) else i}", 1, f"act{i}")
+            if h == 0:
+                acts[i] = rotating([P, S], F32, act_tags[i], 1, f"act{i}")
+            act = acts[i]
             col = N * a + P * t
-            for h in range(2):
-                bank = banks[h]
-                cols = slice(h * N, (h + 1) * N)
-                passes = [(whq[a][0][:, P * t : P * (t + 1)].bitcast(FP8X4), whq[a][1][:, P * t : P * (t + 1)], handq[h][0], handq[h][1][:])]
-                for k in range(2):
-                    passes.append((w4[:, k, 2 * col : 2 * (col + P)].bitcast(FP4X4), w4_plane[:, k, col : col + P], v[k][h], v_plane[k][:, cols]))
-                if h == 1:
-                    passes = passes[::-1]
-                for step, (lhsT, lhsT_scale, rhs, rhs_scale) in enumerate(passes):
-                    nc.tensor.matmul_mx(
-                        out=bank[:], lhsT=lhsT, lhsT_scale=lhsT_scale, rhs=rhs[:].bitcast(FP8X4), rhs_scale=rhs_scale,
-                        start=(step == 0), stop=(step == 2),
-                    )
-                nc.scalar.activation(act[:, cols], bank[:], GELU)
-                if i == 0:
-                    nc.scalar.activation(act[:, cols], act[:, cols], COPY, scale=gains[:, a, t : t + 1])
-            if i > 0:
-                nc.scalar.activation(act[:], act[:], COPY, scale=gains[:, a, t : t + 1])
-            return act
-
-        def scatter(i, act, pieces):
-            width = S // pieces
-            for h in range(pieces):
-                cols = slice(h * width, (h + 1) * width)
-                nc.vector.tensor_tensor(
-                    pages[i][:].indirect(idx3[:, h * width // 16 : (h + 1) * width // 16]), act[:, cols], wgs_rows[i % 4][:, cols], MULT
+            bank = banks[(2 * i + h) % 4]
+            cols = slice(h * N, (h + 1) * N)
+            passes = [(whq[a][0][:, P * t : P * (t + 1)].bitcast(FP8X4), whq[a][1][:, P * t : P * (t + 1)], handq[h][0], handq[h][1][:])]
+            for k in range(2):
+                passes.append((w4[:, k, 2 * col : 2 * (col + P)].bitcast(FP4X4), w4_plane[:, k, col : col + P], v[k][h], v_plane[k][:, cols]))
+            if h == 1 or a == 1:
+                passes = passes[::-1]
+            for step, (lhsT, lhsT_scale, rhs, rhs_scale) in enumerate(passes):
+                nc.tensor.matmul_mx(
+                    out=bank[:], lhsT=lhsT, lhsT_scale=lhsT_scale, rhs=rhs[:].bitcast(FP8X4), rhs_scale=rhs_scale,
+                    start=(step == 0), stop=(step == 2),
                 )
+            nc.scalar.activation(act[:, cols], bank[:], GELU)
+            if i < 2:
+                nc.scalar.activation(act[:, cols], act[:, cols], COPY, scale=gains[:, a, t : t + 1])
+            elif h == 1:
+                nc.scalar.activation(act[:], act[:], COPY, scale=gains[:, a, t : t + 1])
 
-        def round_into_pairs(i, c, pairs):
-            t = i % 4
-            nc.scalar.copy(pairs[:, t // 2, :, t % 2], pages[i][:, c * N : (c + 1) * N])
+        def scatter(i, cols):
+            nc.vector.tensor_tensor(
+                pages[i][:].indirect(idx3[:, cols.start // 16 : cols.stop // 16]), acts[i][:, cols], wgs_rows[i % 4][:, cols], MULT
+            )
 
         def weave(copy, pairs, name, tag="grouped", bufs=4):
             grouped = rotating([P, 4 * N], BF16, tag, bufs, name)
             copy(
                 grouped[:].bitcast(F32).rearrange("p (c u) -> p c u", u=2),
-                pairs[:].rearrange("p u c e -> p u (c e)").bitcast(F32).rearrange("p u c -> p c u"),
+                pairs.rearrange("p u c e -> p u (c e)").bitcast(F32).rearrange("p u c -> p c u"),
             )
             return grouped
-
-        def gather_v2(u, tag):
-            words = rotating([P, 2, S2 // 2], U32, tag, 1, f"v2_{u}")
-            for b in range(2):
-                nc.vector.tensor_copy(words[:, b, :], tab2[b][:].indirect(idx2[:, 16 * u : 16 * u + 16]))
-            return words
 
         def second_product(n, c, a):
             rows = slice(P * n, P * (n + 1))
@@ -221,40 +211,67 @@ def tile_list_drop_move_adviser_kernel(
                 rhs=pageq[a][c][0][:].bitcast(FP8X4), rhs_scale=pageq[a][c][1][:], start=(a == 0), stop=(a == 1),
             )
 
-        ahead = [first_product(i) for i in range(4)]
-        pageq = [[], []]
-        for i in range(8):
-            a, t = divmod(i, 4)
-            scatter(i, ahead[i], 2 if i == 0 else 1)
-            if i == 0:
-                wh_g1 = group_wh(wh_raw[1], rotating([P, 4 * N], BF16, "act0", 1, "wh_g1"))
-            if i == 1:
-                whq.append(quantize(wh_g1, "wh1", rotating([P, N], U32, "act1", 1, "wh1_codes")))
-            if i == 2:
-                v2_plane = rotating([P, S2], U8, "act2", 1, "v2_plane")
-                nc.vector.tensor_copy(v2_plane[:], tab2_plane[:].indirect(idx2[:]))
-            if t == 0:
-                pairs = [rotating([P, 2, N, 2], BF16, "pairs", 4, f"pairs{a}{c}") for c in range(4)]
-            if i < 7:
-                for c in range(4):
-                    round_into_pairs(i, c, pairs[c])
+        halves = [slice(0, N), slice(N, S)]
+        first_product(0, 0)
+        first_product(1, 0)
+        scatter(0, halves[0])
+        scatter(1, halves[0])
+        handq.append(quantize(group_hand(hand_raw[1], "hand_g1"), "hand1"))
+        first_product(0, 1)
+        first_product(1, 1)
+        for i in (2, 3):
+            for h in range(2):
+                first_product(i, h)
+        wh_g1 = group_wh(wh_raw[1], rotating([P, 4 * N], BF16, "grouped", 4, "wh_g1"))
+        scatter(0, halves[1])
+        scatter(1, halves[1])
+        first_pairs = placed.tile([P, 2, T, 2], BF16, name="first_pairs", offset=0, align_bytes=64)
+
+        def round_first(i):
+            nc.scalar.copy(first_pairs[:, i // 2, :, i % 2], pages[i][:])
             if i + 5 < 8:
                 pages.append(load_page(i + 5))
-            if i == 1:
-                ahead.extend([first_product(4), first_product(5)])
-            if i in (2, 4):
-                ahead.append(first_product(len(ahead)))
-            if i == 3:
-                woven = [weave(nc.scalar.copy, pairs[c], f"page_g0{c}") for c in range(4)]
-        caps = []
-        for n, tag in enumerate(("wgs0", "v0", "v1", "wgs1")):
-            caps.append(rotating([P, S], F32, tag, 1, f"cap{n}"))
-            nc.sync.dma_start(caps[n][:], cap[P * n : P * (n + 1), :])
+
+        def round_into_pairs(i, c):
+            t = i % 4
+            nc.scalar.copy(pairs[c][:, t // 2, :, t % 2], pages[i][:, c * N : (c + 1) * N])
+
+        round_first(0)
+        round_first(1)
+        scatter(2, slice(0, S))
+        whq.append(quantize(wh_g1, "wh1", rotating([P, N], U32, "act2", 1, "wh1_codes")))
+        for i in range(4, 8):
+            for h in range(2):
+                first_product(i, h)
+        round_first(2)
+        scatter(3, slice(0, S))
+        v2_plane = rotating([P, S2], U8, "act3", 1, "v2_plane")
+        nc.vector.tensor_copy(v2_plane[:], tab2_plane[:].indirect(idx2[:]))
+        round_first(3)
+        woven = [weave(nc.scalar.copy, first_pairs[:, :, c * N : (c + 1) * N, :], f"page_g0{c}") for c in range(4)]
+        pairs = [rotating([P, 2, N, 2], BF16, "pairs", 4, f"pairs{c}") for c in range(4)]
+        for i in range(4, 8):
+            scatter(i, slice(0, S))
+            if i < 7:
+                for c in range(4):
+                    round_into_pairs(i, c)
+        pageq = [[], []]
+        cap_pair = rotating([P, 2, S], F32, "wgs0", 1, "cap01")
+        nc.sync.dma_start(cap_pair[:], cap[0 : 2 * P, :].rearrange("(n p) m -> p n m", n=2))
+        caps = [cap_pair[:, 0, :], cap_pair[:, 1, :]]
+        cap_pair = placed.tile([P, 2, S], F32, name="cap23", offset=16384, align_bytes=64)
+        nc.sync.dma_start(cap_pair[:], cap[2 * P : 4 * P, :].rearrange("(n p) m -> p n m", n=2))
+        caps.extend([cap_pair[:, 0, :], cap_pair[:, 1, :]])
 
         scores = [rotating([P, T], F32, "page", 5, f"scores{n}") for n in range(4)]
         for c in range(4):
-            round_into_pairs(7, c, pairs[c])
-        v2 = [gather_v2(0, "act0")]
+            round_into_pairs(7, c)
+        v2 = [rotating([P, 2, S2 // 2], U32, "act7", 1, "v2_0")]
+
+        def gather_v2(u, a):
+            nc.vector.tensor_copy(v2[u][:, a, :], tab2[a][:].indirect(idx2[:, 16 * u : 16 * u + 16]))
+
+        gather_v2(0, 0)
         first_codes = rotating([P, 4, N], U32, "wgs2", 1, "page0_codes")
 
         def quantize_and_multiply(a, c, grouped, codes=None):
@@ -265,15 +282,18 @@ def tile_list_drop_move_adviser_kernel(
         last = []
         for c in range(2):
             quantize_and_multiply(0, c, woven[c], first_codes[:, c, :])
-            last.append(weave(nc.vector.tensor_copy, pairs[c], f"page_g1{c}"))
+            last.append(weave(nc.vector.tensor_copy, pairs[c][:], f"page_g1{c}"))
+        gather_v2(0, 1)
         for c in range(2, 4):
-            last.append(weave(nc.scalar.copy, pairs[c], f"page_g1{c}", f"act{c + 3}", 1))
+            last.append(weave(nc.scalar.copy, pairs[c][:], f"page_g1{c}", f"act{c - 2}", 1))
         for c in range(2):
             quantize_and_multiply(1, c, last[c])
             quantize_and_multiply(0, c + 2, woven[c + 2], first_codes[:, c + 2, :])
         for c in range(2, 4):
             quantize_and_multiply(1, c, last[c])
-        v2.append(gather_v2(1, "act6"))
+        v2.append(rotating([P, 2, S2 // 2], U32, "act1", 1, "v2_1"))
+        for a in range(2):
+            gather_v2(1, a)
 
         def cap_and_store(n, cols, picked):
             nc.vector.tensor_tensor(picked[:], picked[:], caps[n][:, cols], MIN)

@@ -75,17 +75,20 @@ def tile_list_drop_move_adviser_kernel(
             nc.sync.dma_start(tile[:], page0.rearrange("(a p t) c -> a t p c", a=2, t=4)[a, t])
             return tile
 
-        def quantize(grouped, name, codes=None):
+        def quantize(grouped, name, codes=None, offset=None):
             if codes is None:
                 codes = keep([P, N], U32, name + "_codes")
-            scales = keep([P, N], U8, name + "_scales")
+            if offset is None:
+                scales = keep([P, N], U8, name + "_scales")
+            else:
+                scales = placed.tile([P, N], U8, name=name + "_scales", offset=offset, align_bytes=64)
             nc.vector.quantize_mx(out=codes[:].bitcast(FP8X4), scales=scales[:], in_=grouped[:])
             return codes, scales
 
         def group_wh(raw, grouped):
             nc.scalar.activation(
-                grouped[:].rearrange("p (t m j) -> p m j t", t=4, j=4),
-                raw[:].rearrange("p j (m t) -> p m j t", t=4),
+                grouped[:].rearrange("p (t m j) -> p m t j", t=4, j=4),
+                raw[:].rearrange("p j (m t) -> p m t j", t=4),
                 COPY,
             )
             return grouped
@@ -93,13 +96,13 @@ def tile_list_drop_move_adviser_kernel(
         def group_hand(raw, name):
             grouped = rotating([P, 4 * N], BF16, "grouped", 4, name)
             nc.scalar.copy(
-                grouped[:].rearrange("p (c i j) -> p c j i", i=4, j=4),
-                raw[:].rearrange("p j (c i) -> p c j i", i=4),
+                grouped[:].rearrange("p (c j) -> p c j", j=4),
+                raw.rearrange("p j c -> p c j"),
             )
             return grouped
 
-        def load_planes_side_by_side(src, name):
-            planes = rotating([P, 2, src.shape[2]], U8, name, 1, name)
+        def load_planes_side_by_side(src, name, offset):
+            planes = placed.tile([P, 2, src.shape[2]], U8, name=name, offset=offset, align_bytes=64)
             nc.vector.memset(planes[:].bitcast(I32), 0)
             for q in range(4):
                 nc.gpsimd.dma_start(
@@ -108,30 +111,31 @@ def tile_list_drop_move_adviser_kernel(
                 )
             return planes
 
-        tab_plane = load_table_scales(nc.gpsimd, tab_scales, "tab_plane")
-        w4_plane_raw = load_planes_side_by_side(w4_scales, "w4_plane_raw")
+        tab_planes = load_planes_side_by_side(tab_scales, "tab_plane", 24576)
+        w4_plane_raw = load_planes_side_by_side(w4_scales, "w4_plane_raw", 24576 + 5120)
         idx = load_list(offs, "idx")
         w4_raw = keep([P, 2, 512], I32, "w4_raw")
         nc.sync.dma_start(w4_raw[:], w4_words.rearrange("k p b -> p k b").bitcast(I32))
-        wh_raw = [load_rows(wh, 0, 0, "wh_raw0")]
-        hand_raw = [load_rows(hand, 0, 1, "hand_raw0")]
+        wh_raw = [load_rows(wh, 0, 2, "wh_raw0")]
+        hand_raw = placed.tile([P, 4, S], F32, name="hand_raw", offset=0, align_bytes=64)
+        nc.sync.dma_start(hand_raw[:], hand.rearrange("(p j) c -> p j c", j=4))
         tab = [load_table_words(tab_words, k, f"tab{k}") for k in range(2)]
         gains = keep([P, 2, 4], F32, "gains")
         nc.sync.dma_start(gains[:], gain.rearrange("(a p t) -> p a t", a=2, t=4))
         idx3 = load_list(offs3, "idx3")
         pages = [load_page(0)]
-        wgs_tiles = [rotating([P, 2, S], F32, f"wgs{t0}", 1, f"wgs{t0}") for t0 in (0, 2)]
-        wgs_rows = [wgs_tiles[t // 2][:, t % 2, :] for t in range(4)]
+        wgs_tiles = [rotating([P, planes, S], F32, f"wgs{t0}", 1, f"wgs{t0}") for t0, planes in ((0, 1), (1, 1), (2, 2))]
+        wgs_rows = [wgs_tiles[0][:, 0, :], wgs_tiles[1][:, 0, :], wgs_tiles[2][:, 0, :], wgs_tiles[2][:, 1, :]]
         load_wgs(wgs_tiles[0], 0, slice(0, N))
-        hand_raw.append(load_rows(hand, 1, 2, "hand_raw1"))
-        pages.append(load_page(1))
         load_wgs(wgs_tiles[0], 0, slice(N, S))
+        pages.append(load_page(1))
+        load_wgs(wgs_tiles[1], 1, slice(0, S))
 
-        v = [[None, None], [None, None]]
+        v_words = [placed.tile([P, S], U32, name=f"v{k}", offset=24576 + 2048 + 4096 * k, align_bytes=64) for k in range(2)]
+        v = [[v_words[k][:, N * h : N * (h + 1)] for h in range(2)] for k in range(2)]
 
-        def gather_v(k, h, tag):
-            v[k][h] = rotating([P, N], U32, tag, 1, f"v{k}{h}")
-            nc.vector.tensor_copy(v[k][h][:], tab[k][:].indirect(idx[:, 32 * h : 32 * h + 32]))
+        def gather_v(k, h):
+            nc.vector.tensor_copy(v[k][h], tab[k][:].indirect(idx[:, 32 * h : 32 * h + 32]))
 
         w4 = keep([P, 2, 2 * H], U8, "w4")
         nc.vector.tensor_copy(
@@ -139,32 +143,33 @@ def tile_list_drop_move_adviser_kernel(
             w4_raw[:].bitcast(U16).rearrange("p k (a m t) -> p (k a) t m", a=2, t=4),
         )
         v_plane = [keep([P, S], U8, f"v_plane{k}") for k in range(2)]
-        nc.vector.memset(v_plane[1][:].bitcast(I32), 0)
-        nc.vector.tensor_copy(v_plane[0][:], tab_plane[:].indirect(idx[:]))
-        nc.gpsimd.dma_start(v_plane[1][0:100, :].bitcast(I32), v_plane[0][4:104, :].bitcast(I32))
+        for k in range(2):
+            nc.vector.tensor_copy(v_plane[k][:], tab_planes[:, k, :].indirect(idx[:]))
+        whq = [quantize(group_wh(wh_raw[0], rotating([P, 4 * N], BF16, "grouped", 4, "wh_g0")), "wh0", offset=24576)]
         w4_plane = keep([P, 2, H], U8, "w4_plane")
         nc.vector.tensor_copy(
             w4_plane[:].rearrange("p k (a t m) -> p (k a) t m", a=2, t=4),
             w4_plane_raw[:].rearrange("p k (a m t) -> p (k a) t m", a=2, t=4),
         )
-        whq = [quantize(group_wh(wh_raw[0], rotating([P, 4 * N], BF16, "grouped", 4, "wh_g0")), "wh0")]
-        gather_v(0, 0, "tab_plane")
-        handq = [quantize(group_hand(hand_raw[0], "hand_g0"), "hand0")]
-        gather_v(1, 0, "w4_plane_raw")
-        gather_v(0, 1, "v01")
-        gather_v(1, 1, "v11")
+        gather_v(0, 0)
+        handq = [quantize(group_hand(hand_raw[:, :, 0:N], "hand_g0"), "hand0", offset=24576 + 512)]
+        gather_v(1, 0)
+        gather_v(0, 1)
+        gather_v(1, 1)
+        handq.append(quantize(group_hand(hand_raw[:, :, N:S], "hand_g1"), "hand1", offset=24576 + 1024))
 
-        wh_raw.append(load_rows(wh, 1, 0, "wh_raw1"))
+        wh_raw.append(load_rows(wh, 1, 2, "wh_raw1"))
         pages.append(load_page(2))
-        load_wgs(wgs_tiles[1], 2, slice(0, S))
+        load_wgs(wgs_tiles[2][:, 0:1, :], 2, slice(0, S))
         pages.append(load_page(3))
+        load_wgs(wgs_tiles[2][:, 1:2, :], 3, slice(0, S))
         idx2 = load_list(offs2, "idx2")
         idx4 = load_list(offs4, "idx4")
         tab2_plane = load_table_scales(nc.sync, tab2_scales, "tab2_plane")
         pages.append(load_page(4))
         tab2 = [load_table_words(tab2_words, a, f"tab2_{a}") for a in range(2)]
 
-        act_tags = ["act0", "act1", "act2", "act3", "act0", "act1", "act6", "act7"]
+        act_tags = ["act0", "act1", "act2", "act3", "act0", "act2", "act6", "act7"]
         acts = {}
 
         def first_product(i, h):
@@ -186,7 +191,7 @@ def tile_list_drop_move_adviser_kernel(
                     start=(step == 0), stop=(step == 2),
                 )
             nc.scalar.activation(act[:, cols], bank[:], GELU)
-            if i < 2:
+            if i == 0:
                 nc.scalar.activation(act[:, cols], act[:, cols], COPY, scale=gains[:, a, t : t + 1])
             elif h == 1:
                 nc.scalar.activation(act[:], act[:], COPY, scale=gains[:, a, t : t + 1])
@@ -212,20 +217,15 @@ def tile_list_drop_move_adviser_kernel(
             )
 
         halves = [slice(0, N), slice(N, S)]
-        first_product(0, 0)
-        first_product(1, 0)
-        scatter(0, halves[0])
-        scatter(1, halves[0])
-        handq.append(quantize(group_hand(hand_raw[1], "hand_g1"), "hand1"))
-        first_product(0, 1)
-        first_product(1, 1)
-        for i in (2, 3):
+        for i in range(4):
             for h in range(2):
                 first_product(i, h)
-        wh_g1 = group_wh(wh_raw[1], rotating([P, 4 * N], BF16, "grouped", 4, "wh_g1"))
+        scatter(0, halves[0])
         scatter(0, halves[1])
-        scatter(1, halves[1])
-        first_pairs = placed.tile([P, 2, T, 2], BF16, name="first_pairs", offset=0, align_bytes=64)
+        wh_g1 = group_wh(wh_raw[1], rotating([P, 4 * N], BF16, "grouped", 4, "wh_g1"))
+        scatter(1, slice(0, S))
+        whq.append(quantize(wh_g1, "wh1", rotating([P, N], U32, "act1", 1, "wh1_codes")))
+        first_pairs = placed.tile([P, 2, T, 2], BF16, name="first_pairs", offset=8192, align_bytes=64)
 
         def round_first(i):
             nc.scalar.copy(first_pairs[:, i // 2, :, i % 2], pages[i][:])
@@ -237,10 +237,11 @@ def tile_list_drop_move_adviser_kernel(
             nc.scalar.copy(pairs[c][:, t // 2, :, t % 2], pages[i][:, c * N : (c + 1) * N])
 
         round_first(0)
+        for h in range(2):
+            first_product(4, h)
         round_first(1)
         scatter(2, slice(0, S))
-        whq.append(quantize(wh_g1, "wh1", rotating([P, N], U32, "act2", 1, "wh1_codes")))
-        for i in range(4, 8):
+        for i in range(5, 8):
             for h in range(2):
                 first_product(i, h)
         round_first(2)
@@ -256,12 +257,9 @@ def tile_list_drop_move_adviser_kernel(
                 for c in range(4):
                     round_into_pairs(i, c)
         pageq = [[], []]
-        cap_pair = rotating([P, 2, S], F32, "wgs0", 1, "cap01")
-        nc.sync.dma_start(cap_pair[:], cap[0 : 2 * P, :].rearrange("(n p) m -> p n m", n=2))
-        caps = [cap_pair[:, 0, :], cap_pair[:, 1, :]]
-        cap_pair = placed.tile([P, 2, S], F32, name="cap23", offset=16384, align_bytes=64)
-        nc.sync.dma_start(cap_pair[:], cap[2 * P : 4 * P, :].rearrange("(n p) m -> p n m", n=2))
-        caps.extend([cap_pair[:, 0, :], cap_pair[:, 1, :]])
+        cap_rows = placed.tile([P, 4, S], F32, name="cap_rows", offset=8192, align_bytes=64)
+        nc.sync.dma_start(cap_rows[:], cap.rearrange("(n p) m -> p n m", n=4))
+        caps = [cap_rows[:, n, :] for n in range(4)]
 
         scores = [rotating([P, T], F32, "page", 5, f"scores{n}") for n in range(4)]
         for c in range(4):

@@ -1,6 +1,7 @@
 from contextlib import ExitStack
 
 import concourse.mybir as mybir
+from concourse.masks import make_identity
 
 F32 = mybir.dt.float32
 BF16 = mybir.dt.bfloat16
@@ -47,27 +48,26 @@ def tile_list_drop_move_adviser_kernel(
             nc.sync.dma_start(lst[:], src)
             return lst
 
-        def load_table_scales(queue, src, name):
-            plane = rotating([P, T], U8, name, 1, name)
+        def load_table_scales(queue, src, plane):
             nc.vector.memset(plane[:].bitcast(I32), 0)
             for q in range(4):
                 queue.dma_start(plane[32 * q : 32 * q + 8, :].bitcast(I32), src[:, 4 * q : 4 * q + 4, :].bitcast(I32))
             return plane
 
-        def load_table_words(src, a, name):
-            words = rotating([P, T], U32, "table", 2, name)
+        def load_table_words(src, a, name, offset):
+            words = placed.tile([P, T], U32, name=name, offset=offset, align_bytes=64)
             nc.sync.dma_start(words[:].bitcast(I32), src[a].rearrange("p t i -> p (t i)").bitcast(I32))
             return words
+
+        def load_w4(a):
+            raw = keep([P, 2, N // 2], I32, f"w4_raw{a}")
+            nc.sync.dma_start(raw[:], w4_words[:, :, 2 * N * a : 2 * N * (a + 1)].rearrange("k p b -> p k b").bitcast(I32))
+            return raw
 
         def load_rows(src, b, place, name):
             raw = placed.tile([P, 4, N], F32, name=name, offset=8192 * place, align_bytes=64)
             nc.sync.dma_start(raw[:], src[:, b * N : (b + 1) * N].rearrange("(p j) c -> p j c", j=4))
             return raw
-
-        def load_wgs(rows, t0, cols):
-            planes = wgs.rearrange("(q t) j -> q t j", t=4)[:, t0 : t0 + rows.shape[1], cols]
-            for q in (0, 2, 1, 3):
-                nc.sync.dma_start(rows[32 * q : 32 * q + 32, :, cols], planes)
 
         def load_page(i):
             a, t = divmod(i, 4)
@@ -96,109 +96,143 @@ def tile_list_drop_move_adviser_kernel(
         def group_hand(raw, name):
             grouped = rotating([P, 4 * N], BF16, "grouped", 4, name)
             nc.scalar.copy(
-                grouped[:].rearrange("p (c j) -> p c j", j=4),
-                raw.rearrange("p j c -> p c j"),
+                grouped[:].rearrange("p (c i j) -> p c j i", i=4, j=4),
+                raw.rearrange("p j (c i) -> p c j i", i=4),
             )
             return grouped
 
         def load_planes_side_by_side(src, name, offset):
             planes = placed.tile([P, 2, src.shape[2]], U8, name=name, offset=offset, align_bytes=64)
             nc.vector.memset(planes[:].bitcast(I32), 0)
-            for q in range(4):
-                nc.gpsimd.dma_start(
+            for q in (0, 2, 1, 3):
+                nc.sync.dma_start(
                     planes[32 * q : 32 * q + 4, :, :].bitcast(I32),
                     src[:, 4 * q : 4 * q + 4, :].rearrange("k r n -> r k n").bitcast(I32),
                 )
             return planes
 
-        tab_planes = load_planes_side_by_side(tab_scales, "tab_plane", 24576)
-        w4_plane_raw = load_planes_side_by_side(w4_scales, "w4_plane_raw", 24576 + 5120)
+        identity = keep([P, P], F32, "identity")
+        make_identity(nc, identity[:])
         idx = load_list(offs, "idx")
-        w4_raw = keep([P, 2, 512], I32, "w4_raw")
-        nc.sync.dma_start(w4_raw[:], w4_words.rearrange("k p b -> p k b").bitcast(I32))
-        wh_raw = [load_rows(wh, 0, 2, "wh_raw0")]
-        hand_raw = placed.tile([P, 4, S], F32, name="hand_raw", offset=0, align_bytes=64)
-        nc.sync.dma_start(hand_raw[:], hand.rearrange("(p j) c -> p j c", j=4))
-        tab = [load_table_words(tab_words, k, f"tab{k}") for k in range(2)]
         gains = keep([P, 2, 4], F32, "gains")
         nc.sync.dma_start(gains[:], gain.rearrange("(a p t) -> p a t", a=2, t=4))
+        wgs_raw = rotating([P, S], F32, "picked", 4, "wgs_raw")
+        nc.sync.dma_start(wgs_raw[:], wgs)
+        w4_raw = [load_w4(0)]
+        tab_plane = load_table_scales(nc.sync, tab_scales, placed.tile([P, T], U8, name="tab_plane", offset=32768 + 1024, align_bytes=64))
+        wh_raw = [load_rows(wh, 0, 2, "wh_raw0")]
+        w4_plane_raw = load_planes_side_by_side(w4_scales, "w4_plane_raw", 32768 + 5120)
+        hand_raw = [load_rows(hand, 0, 0, "hand_raw0")]
+        tab = [load_table_words(tab_words, 0, "tab0", 43520)]
+        tab.append(load_table_words(tab_words, 1, "tab1", 43520 + 8192))
+        v_plane = [keep([P, S], U8, f"v_plane{k}") for k in range(2)]
+        nc.vector.memset(v_plane[1][:].bitcast(I32), 0)
+        nc.vector.tensor_copy(v_plane[0][:], tab_plane[:].indirect(idx[:]))
+        nc.sync.dma_start(v_plane[1][0:100, :].bitcast(I32), v_plane[0][4:104, :].bitcast(I32))
         idx3 = load_list(offs3, "idx3")
         pages = [load_page(0)]
-        wgs_tiles = [rotating([P, planes, S], F32, f"wgs{t0}", 1, f"wgs{t0}") for t0, planes in ((0, 1), (1, 1), (2, 2))]
-        wgs_rows = [wgs_tiles[0][:, 0, :], wgs_tiles[1][:, 0, :], wgs_tiles[2][:, 0, :], wgs_tiles[2][:, 1, :]]
-        load_wgs(wgs_tiles[0], 0, slice(0, N))
-        load_wgs(wgs_tiles[0], 0, slice(N, S))
+        hand_raw.append(load_rows(hand, 1, 1, "hand_raw1"))
         pages.append(load_page(1))
-        load_wgs(wgs_tiles[1], 1, slice(0, S))
+        w4_raw.append(load_w4(1))
 
-        v_words = [placed.tile([P, S], U32, name=f"v{k}", offset=24576 + 2048 + 4096 * k, align_bytes=64) for k in range(2)]
+        def turn_wgs():
+            for jb in range(8):
+                nc.tensor.transpose(banks[4 + jb // 4][:, P * (jb % 4) : P * (jb % 4 + 1)], wgs_raw[:, P * jb : P * (jb + 1)], identity[:])
+
+        turn_wgs()
+        repeated = {}
+
+        def repeat_rows(t):
+            if t < 2:
+                repeated[t] = rotating([P, 8, 4, 32], F32, "pairs", 4, f"repeated{t}")
+            else:
+                repeated[t] = placed.tile([P, 8, 4, 32], F32, name=f"repeated{t}", offset=4096 * t, align_bytes=64)
+            for h in range(2):
+                rows_of_t = banks[4 + h][:].rearrange("p (b q t) -> p b t q", b=4, t=4)[:, :, t : t + 1, :]
+                nc.scalar.copy(repeated[t][:, 4 * h : 4 * h + 4, :, :], rows_of_t.to_broadcast([P, 4, 4, 32]))
+
+        weights = {}
+
+        def make_weights(i):
+            a, t = divmod(i, 4)
+            weights[i] = rotating([P, S], F32, "last_weights", 1, "weights7") if i == 7 else rotating([P, S], F32, "weights", 4, f"weights{i}")
+            for h in range(2):
+                bank = banks[6 + h]
+                for b in range(4):
+                    nc.tensor.transpose(bank[:, P * b : P * (b + 1)], repeated[t][:, 4 * h + b, :, :].rearrange("p g q -> p (g q)"), identity[:])
+                nc.scalar.activation(weights[i][:, h * N : (h + 1) * N], bank[:], COPY, scale=gains[:, a, t : t + 1])
+
+        repeat_rows(0)
+
+        v_words = [placed.tile([P, S], U32, name=f"v{k}", offset=32768 + 2048 + 4608 * k, align_bytes=64) for k in range(2)]
         v = [[v_words[k][:, N * h : N * (h + 1)] for h in range(2)] for k in range(2)]
 
         def gather_v(k, h):
             nc.vector.tensor_copy(v[k][h], tab[k][:].indirect(idx[:, 32 * h : 32 * h + 32]))
 
-        w4 = keep([P, 2, 2 * H], U8, "w4")
-        nc.vector.tensor_copy(
-            w4[:].bitcast(U16).rearrange("p k (a t m) -> p (k a) t m", a=2, t=4),
-            w4_raw[:].bitcast(U16).rearrange("p k (a m t) -> p (k a) t m", a=2, t=4),
-        )
-        v_plane = [keep([P, S], U8, f"v_plane{k}") for k in range(2)]
-        for k in range(2):
-            nc.vector.tensor_copy(v_plane[k][:], tab_planes[:, k, :].indirect(idx[:]))
-        whq = [quantize(group_wh(wh_raw[0], rotating([P, 4 * N], BF16, "grouped", 4, "wh_g0")), "wh0", offset=24576)]
+        def permute_w4(a, words):
+            nc.vector.tensor_copy(
+                words[:].bitcast(U16).rearrange("p k (t m) -> p k t m", t=4),
+                w4_raw[a][:].bitcast(U16).rearrange("p k (m t) -> p k t m", t=4),
+            )
+            return words
+
+        w4 = [permute_w4(0, keep([P, 2, 2 * N], U8, "w4_0"))]
+        whq = [quantize(group_wh(wh_raw[0], rotating([P, 4 * N], BF16, "grouped", 4, "wh_g0")), "wh0", offset=32768 + 1024)]
         w4_plane = keep([P, 2, H], U8, "w4_plane")
         nc.vector.tensor_copy(
             w4_plane[:].rearrange("p k (a t m) -> p (k a) t m", a=2, t=4),
             w4_plane_raw[:].rearrange("p k (a m t) -> p (k a) t m", a=2, t=4),
         )
         gather_v(0, 0)
-        handq = [quantize(group_hand(hand_raw[:, :, 0:N], "hand_g0"), "hand0", offset=24576 + 512)]
-        gather_v(1, 0)
         gather_v(0, 1)
+        handq = [quantize(group_hand(hand_raw[0][:], "hand_g0"), "hand0", offset=32768 + 6144)]
+        make_weights(0)
+        repeat_rows(1)
+        make_weights(1)
+        gather_v(1, 0)
         gather_v(1, 1)
-        handq.append(quantize(group_hand(hand_raw[:, :, N:S], "hand_g1"), "hand1", offset=24576 + 1024))
 
         wh_raw.append(load_rows(wh, 1, 2, "wh_raw1"))
         pages.append(load_page(2))
-        load_wgs(wgs_tiles[2][:, 0:1, :], 2, slice(0, S))
         pages.append(load_page(3))
-        load_wgs(wgs_tiles[2][:, 1:2, :], 3, slice(0, S))
         idx2 = load_list(offs2, "idx2")
         idx4 = load_list(offs4, "idx4")
-        tab2_plane = load_table_scales(nc.sync, tab2_scales, "tab2_plane")
+        tab2_plane = load_table_scales(nc.sync, tab2_scales, keep([P, T], U8, "tab2_plane"))
         pages.append(load_page(4))
-        tab2 = [load_table_words(tab2_words, a, f"tab2_{a}") for a in range(2)]
+        tab2 = [load_table_words(tab2_words, a, f"tab2_{a}", 43520 + 8192 * a) for a in range(2)]
 
-        act_tags = ["act0", "act1", "act2", "act3", "act0", "act2", "act6", "act7"]
+        act_tags = ["act0", "act1", "act2", "act3", "act4", "act2", "act6", "act7"]
         acts = {}
+        acts_done = []
 
         def first_product(i, h):
             a, t = divmod(i, 4)
-            if h == 0:
+            if i not in acts:
                 acts[i] = rotating([P, S], F32, act_tags[i], 1, f"act{i}")
             act = acts[i]
             col = N * a + P * t
-            bank = banks[(2 * i + h) % 4]
+            bank = banks[4 + i] if i < 2 and h == 0 else banks[len(acts_done) % 4]
             cols = slice(h * N, (h + 1) * N)
             passes = [(whq[a][0][:, P * t : P * (t + 1)].bitcast(FP8X4), whq[a][1][:, P * t : P * (t + 1)], handq[h][0], handq[h][1][:])]
             for k in range(2):
-                passes.append((w4[:, k, 2 * col : 2 * (col + P)].bitcast(FP4X4), w4_plane[:, k, col : col + P], v[k][h], v_plane[k][:, cols]))
-            if h == 1 or a == 1:
+                passes.append((w4[a][:, k, 2 * P * t : 2 * P * (t + 1)].bitcast(FP4X4), w4_plane[:, k, col : col + P], v[k][h], v_plane[k][:, cols]))
+            if h == 1 or i > 0:
                 passes = passes[::-1]
+            else:
+                passes = [passes[1], passes[0], passes[2]]
             for step, (lhsT, lhsT_scale, rhs, rhs_scale) in enumerate(passes):
                 nc.tensor.matmul_mx(
                     out=bank[:], lhsT=lhsT, lhsT_scale=lhsT_scale, rhs=rhs[:].bitcast(FP8X4), rhs_scale=rhs_scale,
                     start=(step == 0), stop=(step == 2),
                 )
             nc.scalar.activation(act[:, cols], bank[:], GELU)
-            if i == 0:
-                nc.scalar.activation(act[:, cols], act[:, cols], COPY, scale=gains[:, a, t : t + 1])
-            elif h == 1:
-                nc.scalar.activation(act[:], act[:], COPY, scale=gains[:, a, t : t + 1])
+            if i >= 2 or h == 1:
+                acts_done.append((i, h))
 
         def scatter(i, cols):
             nc.vector.tensor_tensor(
-                pages[i][:].indirect(idx3[:, cols.start // 16 : cols.stop // 16]), acts[i][:, cols], wgs_rows[i % 4][:, cols], MULT
+                pages[i][:].indirect(idx3[:, cols.start // 16 : cols.stop // 16]), acts[i][:, cols], weights[i][:, cols], MULT
             )
 
         def weave(copy, pairs, name, tag="grouped", bufs=4):
@@ -217,15 +251,26 @@ def tile_list_drop_move_adviser_kernel(
             )
 
         halves = [slice(0, N), slice(N, S)]
-        for i in range(4):
-            for h in range(2):
-                first_product(i, h)
+        first_product(0, 0)
+        first_product(1, 0)
         scatter(0, halves[0])
-        scatter(0, halves[1])
+        handq.append(quantize(group_hand(hand_raw[1][:], "hand_g1"), "hand1"))
+        scatter(1, halves[0])
+        first_product(0, 1)
+        first_product(1, 1)
         wh_g1 = group_wh(wh_raw[1], rotating([P, 4 * N], BF16, "grouped", 4, "wh_g1"))
-        scatter(1, slice(0, S))
+        turn_wgs()
+        for h in (1, 0):
+            for i in (2, 3):
+                first_product(i, h)
+        for i in (2, 3):
+            repeat_rows(i)
+            make_weights(i)
+        scatter(0, halves[1])
+        w4.append(permute_w4(1, rotating([P, 2, 2 * N], U8, "act0", 1, "w4_1")))
+        scatter(1, halves[1])
         whq.append(quantize(wh_g1, "wh1", rotating([P, N], U32, "act1", 1, "wh1_codes")))
-        first_pairs = placed.tile([P, 2, T, 2], BF16, name="first_pairs", offset=8192, align_bytes=64)
+        first_pairs = placed.tile([P, 2, T, 2], BF16, name="first_pairs", offset=16384, align_bytes=64)
 
         def round_first(i):
             nc.scalar.copy(first_pairs[:, i // 2, :, i % 2], pages[i][:])
@@ -239,11 +284,13 @@ def tile_list_drop_move_adviser_kernel(
         round_first(0)
         for h in range(2):
             first_product(4, h)
+        make_weights(4)
         round_first(1)
         scatter(2, slice(0, S))
         for i in range(5, 8):
             for h in range(2):
                 first_product(i, h)
+            make_weights(i)
         round_first(2)
         scatter(3, slice(0, S))
         v2_plane = rotating([P, S2], U8, "act3", 1, "v2_plane")
@@ -257,7 +304,7 @@ def tile_list_drop_move_adviser_kernel(
                 for c in range(4):
                     round_into_pairs(i, c)
         pageq = [[], []]
-        cap_rows = placed.tile([P, 4, S], F32, name="cap_rows", offset=8192, align_bytes=64)
+        cap_rows = placed.tile([P, 4, S], F32, name="cap_rows", offset=16384, align_bytes=64)
         nc.sync.dma_start(cap_rows[:], cap.rearrange("(n p) m -> p n m", n=4))
         caps = [cap_rows[:, n, :] for n in range(4)]
 
@@ -270,7 +317,7 @@ def tile_list_drop_move_adviser_kernel(
             nc.vector.tensor_copy(v2[u][:, a, :], tab2[a][:].indirect(idx2[:, 16 * u : 16 * u + 16]))
 
         gather_v2(0, 0)
-        first_codes = rotating([P, 4, N], U32, "wgs2", 1, "page0_codes")
+        first_codes = rotating([P, 4, N], U32, "last_weights", 1, "page0_codes")
 
         def quantize_and_multiply(a, c, grouped, codes=None):
             pageq[a].append(quantize(grouped, f"page{a}{c}", codes))
@@ -283,7 +330,7 @@ def tile_list_drop_move_adviser_kernel(
             last.append(weave(nc.vector.tensor_copy, pairs[c][:], f"page_g1{c}"))
         gather_v2(0, 1)
         for c in range(2, 4):
-            last.append(weave(nc.scalar.copy, pairs[c][:], f"page_g1{c}", f"act{c - 2}", 1))
+            last.append(weave(nc.scalar.copy, pairs[c][:], f"page_g1{c}", ("act4", "act1")[c - 2], 1))
         for c in range(2):
             quantize_and_multiply(1, c, last[c])
             quantize_and_multiply(0, c + 2, woven[c + 2], first_codes[:, c + 2, :])

@@ -22,7 +22,18 @@ S = 1024
 S2 = 512
 H = 1024
 N = 512
+QUARTER = 256
+KB = 1024
 FLOPS = 5368709120
+
+TABLE_AT = 0
+HAND_AT = 16 * KB
+WH_AT = 32 * KB
+GROUPED_AT = 48 * KB
+TURNED_AT = 64 * KB
+ACT_AT = 80 * KB
+WEIGHTS_AT = 96 * KB
+PAGE_AT = 112 * KB
 
 
 def tile_list_drop_move_adviser_kernel(
@@ -32,7 +43,6 @@ def tile_list_drop_move_adviser_kernel(
     nc = tc.nc
     with ExitStack() as ctx:
         held = ctx.enter_context(tc.tile_pool(name="held", bufs=1))
-        ring = ctx.enter_context(tc.tile_pool(name="ring", bufs=1))
         placed = ctx.enter_context(tc.tile_pool(name="placed", bufs=1))
         psum = ctx.enter_context(tc.psum_pool(name="psum", bufs=1))
         banks = [psum.tile([P, N], F32, name=f"bank{b}") for b in range(8)]
@@ -40,320 +50,361 @@ def tile_list_drop_move_adviser_kernel(
         def keep(shape, dtype, name):
             return held.tile(shape, dtype, name=name, align_bytes=64)
 
-        def rotating(shape, dtype, tag, bufs, name):
-            return ring.tile(shape, dtype, name=name, tag=tag, bufs=bufs, align_bytes=64)
+        def place(shape, dtype, name, offset):
+            return placed.tile(shape, dtype, name=name, offset=offset, align_bytes=64)
 
         def load_list(src, name):
             lst = held.tile(list(src.shape), U16, name=name)
             nc.sync.dma_start(lst[:], src)
             return lst
 
-        def load_table_scales(queue, src, plane):
-            nc.vector.memset(plane[:].bitcast(I32), 0)
-            for q in range(4):
-                queue.dma_start(plane[32 * q : 32 * q + 8, :].bitcast(I32), src[:, 4 * q : 4 * q + 4, :].bitcast(I32))
-            return plane
-
-        def load_table_words(src, a, name, offset):
-            words = placed.tile([P, T], U32, name=name, offset=offset, align_bytes=64)
-            nc.sync.dma_start(words[:].bitcast(I32), src[a].rearrange("p t i -> p (t i)").bitcast(I32))
-            return words
-
-        def load_w4(a):
-            raw = keep([P, 2, N // 2], I32, f"w4_raw{a}")
-            nc.sync.dma_start(raw[:], w4_words[:, :, 2 * N * a : 2 * N * (a + 1)].rearrange("k p b -> p k b").bitcast(I32))
-            return raw
-
-        def load_rows(src, b, place, name):
-            raw = placed.tile([P, 4, N], F32, name=name, offset=8192 * place, align_bytes=64)
-            nc.sync.dma_start(raw[:], src[:, b * N : (b + 1) * N].rearrange("(p j) c -> p j c", j=4))
-            return raw
-
-        def load_page(i):
-            a, t = divmod(i, 4)
-            tile = rotating([P, T], F32, "page", 5, f"page{i}")
-            nc.sync.dma_start(tile[:], page0.rearrange("(a p t) c -> a t p c", a=2, t=4)[a, t])
-            return tile
-
-        def quantize(grouped, name, codes=None, offset=None):
-            if codes is None:
-                codes = keep([P, N], U32, name + "_codes")
-            if offset is None:
-                scales = keep([P, N], U8, name + "_scales")
-            else:
-                scales = placed.tile([P, N], U8, name=name + "_scales", offset=offset, align_bytes=64)
-            nc.vector.quantize_mx(out=codes[:].bitcast(FP8X4), scales=scales[:], in_=grouped[:])
-            return codes, scales
-
-        def group_wh(raw, grouped):
-            nc.scalar.activation(
-                grouped[:].rearrange("p (t m j) -> p m t j", t=4, j=4),
-                raw[:].rearrange("p j (m t) -> p m t j", t=4),
-                COPY,
-            )
-            return grouped
-
-        def group_hand(raw, name):
-            grouped = rotating([P, 4 * N], BF16, "grouped", 4, name)
-            nc.scalar.copy(
-                grouped[:].rearrange("p (c i j) -> p c j i", i=4, j=4),
-                raw.rearrange("p j (c i) -> p c j i", i=4),
-            )
-            return grouped
-
-        def load_planes_side_by_side(src, name, offset):
-            planes = placed.tile([P, 2, src.shape[2]], U8, name=name, offset=offset, align_bytes=64)
-            nc.vector.memset(planes[:].bitcast(I32), 0)
+        def load_planes_side_by_side(src, planes):
             for q in (0, 2, 1, 3):
                 nc.sync.dma_start(
                     planes[32 * q : 32 * q + 4, :, :].bitcast(I32),
                     src[:, 4 * q : 4 * q + 4, :].rearrange("k r n -> r k n").bitcast(I32),
                 )
-            return planes
 
-        identity = keep([P, P], F32, "identity")
-        make_identity(nc, identity[:])
-        idx = load_list(offs, "idx")
-        gains = keep([P, 2, 4], F32, "gains")
-        nc.sync.dma_start(gains[:], gain.rearrange("(a p t) -> p a t", a=2, t=4))
-        wgs_raw = rotating([P, S], F32, "picked", 4, "wgs_raw")
-        nc.sync.dma_start(wgs_raw[:], wgs)
-        w4_raw = [load_w4(0)]
-        tab_plane = load_table_scales(nc.sync, tab_scales, placed.tile([P, T], U8, name="tab_plane", offset=32768 + 1024, align_bytes=64))
-        wh_raw = [load_rows(wh, 0, 2, "wh_raw0")]
-        w4_plane_raw = load_planes_side_by_side(w4_scales, "w4_plane_raw", 32768 + 5120)
-        hand_raw = [load_rows(hand, 0, 0, "hand_raw0")]
-        tab = [load_table_words(tab_words, 0, "tab0", 43520)]
-        tab.append(load_table_words(tab_words, 1, "tab1", 43520 + 8192))
-        v_plane = [keep([P, S], U8, f"v_plane{k}") for k in range(2)]
-        nc.vector.memset(v_plane[1][:].bitcast(I32), 0)
-        nc.vector.tensor_copy(v_plane[0][:], tab_plane[:].indirect(idx[:]))
-        nc.sync.dma_start(v_plane[1][0:100, :].bitcast(I32), v_plane[0][4:104, :].bitcast(I32))
-        idx3 = load_list(offs3, "idx3")
-        pages = [load_page(0)]
-        hand_raw.append(load_rows(hand, 1, 1, "hand_raw1"))
-        pages.append(load_page(1))
-        w4_raw.append(load_w4(1))
+        def load_planes_stacked(src, plane):
+            for q in range(4):
+                nc.sync.dma_start(plane[32 * q : 32 * q + 8, :].bitcast(I32), src[:, 4 * q : 4 * q + 4, :].bitcast(I32))
 
-        def turn_wgs():
-            for jb in range(8):
-                nc.tensor.transpose(banks[4 + jb // 4][:, P * (jb % 4) : P * (jb % 4 + 1)], wgs_raw[:, P * jb : P * (jb + 1)], identity[:])
-
-        turn_wgs()
-        repeated = {}
-
-        def repeat_rows(t):
-            if t < 2:
-                repeated[t] = rotating([P, 8, 4, 32], F32, "pairs", 4, f"repeated{t}")
-            else:
-                repeated[t] = placed.tile([P, 8, 4, 32], F32, name=f"repeated{t}", offset=4096 * t, align_bytes=64)
-            for h in range(2):
-                rows_of_t = banks[4 + h][:].rearrange("p (b q t) -> p b t q", b=4, t=4)[:, :, t : t + 1, :]
-                nc.scalar.copy(repeated[t][:, 4 * h : 4 * h + 4, :, :], rows_of_t.to_broadcast([P, 4, 4, 32]))
-
-        weights = {}
-
-        def make_weights(i):
-            a, t = divmod(i, 4)
-            weights[i] = rotating([P, S], F32, "last_weights", 1, "weights7") if i == 7 else rotating([P, S], F32, "weights", 4, f"weights{i}")
-            for h in range(2):
-                bank = banks[6 + h]
-                for b in range(4):
-                    nc.tensor.transpose(bank[:, P * b : P * (b + 1)], repeated[t][:, 4 * h + b, :, :].rearrange("p g q -> p (g q)"), identity[:])
-                nc.scalar.activation(weights[i][:, h * N : (h + 1) * N], bank[:], COPY, scale=gains[:, a, t : t + 1])
-
-        repeat_rows(0)
-
-        v_words = [placed.tile([P, S], U32, name=f"v{k}", offset=32768 + 2048 + 4608 * k, align_bytes=64) for k in range(2)]
-        v = [[v_words[k][:, N * h : N * (h + 1)] for h in range(2)] for k in range(2)]
-
-        def gather_v(k, h):
-            nc.vector.tensor_copy(v[k][h], tab[k][:].indirect(idx[:, 32 * h : 32 * h + 32]))
-
-        def permute_w4(a, words):
-            nc.vector.tensor_copy(
-                words[:].bitcast(U16).rearrange("p k (t m) -> p k t m", t=4),
-                w4_raw[a][:].bitcast(U16).rearrange("p k (m t) -> p k t m", t=4),
-            )
+        def load_table_words(src, a, name):
+            words = place([P, T], U32, name, TABLE_AT + 8 * KB * a)
+            nc.sync.dma_start(words[:].bitcast(I32), src[a].rearrange("p t i -> p (t i)").bitcast(I32))
             return words
 
-        w4 = [permute_w4(0, keep([P, 2, 2 * N], U8, "w4_0"))]
-        whq = [quantize(group_wh(wh_raw[0], rotating([P, 4 * N], BF16, "grouped", 4, "wh_g0")), "wh0", offset=32768 + 1024)]
-        w4_plane = keep([P, 2, H], U8, "w4_plane")
-        nc.vector.tensor_copy(
-            w4_plane[:].rearrange("p k (a t m) -> p (k a) t m", a=2, t=4),
-            w4_plane_raw[:].rearrange("p k (a m t) -> p (k a) t m", a=2, t=4),
-        )
-        gather_v(0, 0)
-        gather_v(0, 1)
-        handq = [quantize(group_hand(hand_raw[0][:], "hand_g0"), "hand0", offset=32768 + 6144)]
-        make_weights(0)
-        repeat_rows(1)
-        make_weights(1)
-        gather_v(1, 0)
-        gather_v(1, 1)
+        def load_w4(lo, hi):
+            words = keep([P, 2, 2 * (hi - lo)], U8, f"w4_{lo}")
+            nc.sync.dma_start(words[:].bitcast(I32), w4_words[:, :, 2 * lo : 2 * hi].rearrange("k p b -> p k b").bitcast(I32))
+            return words
 
-        wh_raw.append(load_rows(wh, 1, 2, "wh_raw1"))
-        pages.append(load_page(2))
-        pages.append(load_page(3))
-        idx2 = load_list(offs2, "idx2")
-        idx4 = load_list(offs4, "idx4")
-        tab2_plane = load_table_scales(nc.sync, tab2_scales, keep([P, T], U8, "tab2_plane"))
-        pages.append(load_page(4))
-        tab2 = [load_table_words(tab2_words, a, f"tab2_{a}", 43520 + 8192 * a) for a in range(2)]
+        def load_rows(src, lo, hi, offset, name):
+            raw = place([P, 4, hi - lo], F32, name, offset)
+            nc.sync.dma_start(raw[:], src[:, lo:hi].rearrange("(p j) c -> p j c", j=4))
+            return raw
 
-        act_tags = ["act0", "act1", "act2", "act3", "act4", "act2", "act6", "act7"]
-        acts = {}
-        acts_done = []
+        def load_page(i):
+            tile = place([P, T], F32, f"page{i}", PAGE_AT + 8 * KB * i)
+            rows = page0[P * i : P * (i + 1), :] if i < 4 else page0[N:H, :].rearrange("(p t) c -> t p c", t=4)[i - 4]
+            nc.sync.dma_start(tile[:], rows)
+            return tile
 
-        def first_product(i, h):
-            a, t = divmod(i, 4)
-            if i not in acts:
-                acts[i] = rotating([P, S], F32, act_tags[i], 1, f"act{i}")
-            act = acts[i]
-            col = N * a + P * t
-            bank = banks[4 + i] if i < 2 and h == 0 else banks[len(acts_done) % 4]
-            cols = slice(h * N, (h + 1) * N)
-            passes = [(whq[a][0][:, P * t : P * (t + 1)].bitcast(FP8X4), whq[a][1][:, P * t : P * (t + 1)], handq[h][0], handq[h][1][:])]
-            for k in range(2):
-                passes.append((w4[a][:, k, 2 * P * t : 2 * P * (t + 1)].bitcast(FP4X4), w4_plane[:, k, col : col + P], v[k][h], v_plane[k][:, cols]))
-            if h == 1 or i > 0:
-                passes = passes[::-1]
-            else:
-                passes = [passes[1], passes[0], passes[2]]
-            for step, (lhsT, lhsT_scale, rhs, rhs_scale) in enumerate(passes):
-                nc.tensor.matmul_mx(
-                    out=bank[:], lhsT=lhsT, lhsT_scale=lhsT_scale, rhs=rhs[:].bitcast(FP8X4), rhs_scale=rhs_scale,
-                    start=(step == 0), stop=(step == 2),
-                )
-            nc.scalar.activation(act[:, cols], bank[:], GELU)
-            if i >= 2 or h == 1:
-                acts_done.append((i, h))
-
-        def scatter(i, cols):
-            nc.vector.tensor_tensor(
-                pages[i][:].indirect(idx3[:, cols.start // 16 : cols.stop // 16]), acts[i][:, cols], weights[i][:, cols], MULT
-            )
-
-        def weave(copy, pairs, name, tag="grouped", bufs=4):
-            grouped = rotating([P, 4 * N], BF16, tag, bufs, name)
-            copy(
-                grouped[:].bitcast(F32).rearrange("p (c u) -> p c u", u=2),
-                pairs.rearrange("p u c e -> p u (c e)").bitcast(F32).rearrange("p u c -> p c u"),
+        def group(raw, name, offset):
+            grouped = place([P, 4 * raw.shape[2]], BF16, name, offset)
+            nc.scalar.copy(
+                grouped[:].rearrange("p (c i j) -> p c j i", i=4, j=4),
+                raw[:].rearrange("p j (c i) -> p c j i", i=4),
             )
             return grouped
 
-        def second_product(n, c, a):
-            rows = slice(P * n, P * (n + 1))
-            nc.tensor.matmul_mx(
-                out=banks[4 * ((n + 1) % 2) + c][:], lhsT=v2[n // 2][:, a, P * (n % 2) : P * (n % 2 + 1)].bitcast(FP8X4), lhsT_scale=v2_plane[4 * a : P, rows],
-                rhs=pageq[a][c][0][:].bitcast(FP8X4), rhs_scale=pageq[a][c][1][:], start=(a == 0), stop=(a == 1),
+        def quantize(grouped, name, scales=None):
+            width = grouped.shape[1] // 4
+            codes = keep([P, width], U32, name + "_codes")
+            if scales is None:
+                scales = keep([P, width], U8, name + "_scales")
+            nc.vector.quantize_mx(out=codes[:].bitcast(FP8X4), scales=scales[:], in_=grouped[:])
+            return codes, scales
+
+        wh_edges = [0, 256, 512, H]
+        w4_edges = [0, 256, H]
+
+        def piece(edges, col):
+            return max(n for n in range(len(edges) - 1) if edges[n] <= col)
+
+        tab_planes = keep([P, 2, T], U8, "tab_planes")
+        w4_planes = keep([P, 2, H], U8, "w4_planes")
+        tab2_plane = keep([P, T], U8, "tab2_plane")
+        gain_rows = keep([P, P], F32, "gain_rows")
+        nc.vector.memset(tab_planes[:].bitcast(I32), 0)
+        nc.vector.memset(w4_planes[:].bitcast(I32), 0)
+        nc.vector.memset(gain_rows[:], 0.0)
+        nc.vector.memset(tab2_plane[:].bitcast(I32), 0)
+        identity = keep([P, P], F32, "identity")
+        make_identity(nc, identity[:])
+
+        table_warm_up = keep([P, 1], F32, "table_warm_up")
+        nc.scalar.activation(table_warm_up[:], identity[:, 0:1], GELU)
+
+        def load_wgs(h):
+            rows = keep([P, N], F32, f"wgs{h}")
+            nc.sync.dma_start(rows[:], wgs[:, N * h : N * (h + 1)])
+            return rows
+
+        def load_hand(q):
+            return load_rows(hand, QUARTER * q, QUARTER * (q + 1), HAND_AT + 4 * KB * q, f"hand_raw{q}")
+
+        idx = load_list(offs, "idx")
+        tab = [load_table_words(tab_words, 0, "tab0")]
+        w4 = [load_w4(0, 256)]
+        idx3 = load_list(offs3, "idx3")
+        load_planes_side_by_side(tab_scales, tab_planes)
+        nc.sync.dma_start(gain_rows[0:4, :], gain[0:N].rearrange("(c m) -> c m", m=P))
+        wh_raw = [load_rows(wh, 0, 256, WH_AT, "wh_raw0")]
+        hand_raw = [load_hand(0), load_hand(1)]
+        tab.append(load_table_words(tab_words, 1, "tab1"))
+        load_planes_side_by_side(w4_scales, w4_planes)
+        wgs_rows = [load_wgs(0)]
+        pages = [load_page(0)]
+        hand_raw.append(load_hand(2))
+        pages.append(load_page(1))
+        hand_raw.append(load_hand(3))
+        wgs_rows.append(load_wgs(1))
+        wh_raw.append(load_rows(wh, 256, 512, WH_AT + 4 * KB, "wh_raw1"))
+        wh_raw.append(load_rows(wh, 512, H, WH_AT + 8 * KB, "wh_raw2"))
+        w4.append(load_w4(256, H))
+        pages.append(load_page(2))
+        pages.append(load_page(3))
+        pages.append(load_page(4))
+        idx2 = load_list(offs2, "idx2")
+        idx4 = load_list(offs4, "idx4")
+        dealt_gains = keep([P, 4], F32, "dealt_gains")
+        nc.sync.dma_start(dealt_gains[:], gain[N:H].rearrange("(p t) -> p t", t=4))
+        weights = {}
+
+        def load_dealt_wgs(i):
+            weights[i, 0] = place([P, S], F32, f"weights{i}", WEIGHTS_AT + 4 * KB * (i % 4))
+            for q in range(4):
+                nc.sync.dma_start(weights[i, 0][32 * q : 32 * (q + 1), :], wgs.rearrange("(m t) c -> t m c", t=4)[i - 4])
+
+        load_dealt_wgs(4)
+        load_dealt_wgs(5)
+        load_planes_stacked(tab2_scales, tab2_plane)
+        pages.append(load_page(5))
+
+        gains = {}
+
+        def turn_gains(lo, hi, bank):
+            nc.tensor.transpose(bank[:, 0:P], gain_rows[:], identity[:])
+            turned_gains = keep([P, hi - lo], F32, f"gains{lo}")
+            nc.scalar.copy(turned_gains[:], bank[:, lo:hi])
+            for i in range(lo, hi):
+                gains[i] = turned_gains[:, i - lo : i - lo + 1]
+
+        turn_gains(0, 2, banks[0])
+
+        v = [[keep([P, N], U32, "v00"), keep([P, N], U32, "v01")], [keep([P, N], U32, "v10"), keep([P, N], U32, "v11")]]
+        v_plane = [keep([P, S], U8, f"v_plane{k}") for k in range(2)]
+
+        def gather_v(k, h):
+            nc.vector.tensor_copy(v[k][h][:], tab[k][:].indirect(idx[:, 32 * h : 32 * (h + 1)]))
+
+        def group_wh(n, offset):
+            return group(wh_raw[n], f"wh_g{n}", offset)
+
+        def group_hand(q):
+            return group(hand_raw[q], f"hand_g{q}", GROUPED_AT + 2 * KB * q)
+
+        acts = {}
+        sums = []
+
+        def make_weights(i, lo, hi, offset):
+            weights[i, lo] = place([P, hi - lo], F32, f"weights{i}_{lo}", offset)
+            for h in range(lo // N, (hi - 1) // N + 1):
+                first, last = max(lo, N * h), min(hi, N * (h + 1))
+                nc.scalar.activation(weights[i, lo][:, first - lo : last - lo], wgs_rows[h][:, first - N * h : last - N * h], COPY, scale=gains[i])
+
+        def first_product(i, lo, hi, act):
+            bank = banks[4 + len(sums) % 4]
+            if (i, lo) != (0, 0):
+                sums.append((i, lo))
+            n4 = piece(w4_edges, P * i)
+            at4 = P * i - w4_edges[n4]
+            nh = piece(wh_edges, P * i)
+            ath = P * i - wh_edges[nh]
+            width = N if hi - lo == N else P
+            table_passes = [
+                (at, width, w4[n4][:, k, 2 * at4 : 2 * (at4 + P)].bitcast(FP4X4), w4_planes[:, k, P * i : P * (i + 1)],
+                 v[k][at // N][:, at % N : at % N + width], v_plane[k][:, at : at + width])
+                for k in range(2) for at in range(lo, hi, width)
+            ]
+            hand_passes = [
+                (at, QUARTER, whq[nh][0][:, ath : ath + P].bitcast(FP8X4), whq[nh][1][:, ath : ath + P],
+                 handq[at // QUARTER][0][:], handq[at // QUARTER][1][:])
+                for at in range(lo, hi, QUARTER)
+            ]
+            passes = table_passes + hand_passes if (i, lo) != (0, 0) else table_passes[:1] + hand_passes + table_passes[1:]
+            for step, (at, cols, lhsT, lhsT_scale, rhs, rhs_scale) in enumerate(passes):
+                nc.tensor.matmul_mx(
+                    out=bank[:, at - lo : at - lo + cols], lhsT=lhsT, lhsT_scale=lhsT_scale, rhs=rhs.bitcast(FP8X4), rhs_scale=rhs_scale,
+                    start=(step == 0), stop=(step == len(passes) - 1),
+                )
+            nc.scalar.activation(act, bank[:, 0 : hi - lo], GELU)
+
+        def whole_tile(i):
+            make_weights(i, 0, S, WEIGHTS_AT + 4 * KB * (i % 4))
+            acts[i, 0] = place([P, S], F32, f"act{i}", ACT_AT + 4 * KB * (i % 4))
+            for h in range(2):
+                first_product(i, N * h, N * (h + 1), acts[i, 0][:, h * N : (h + 1) * N])
+
+        def part_tile(i, lo, hi, offset):
+            acts[i, lo] = place([P, hi - lo], F32, f"act{i}_{lo}", offset)
+            first_product(i, lo, hi, acts[i, lo][:])
+
+        def scatter(i, lo, hi):
+            nc.vector.tensor_tensor(pages[i][:].indirect(idx3[:, lo // 16 : hi // 16]), acts[i, lo][:], weights[i, lo][:], MULT)
+
+        turned = [place([P, 4, 2, P, 2], BF16, f"turned{c}", HAND_AT + 4 * KB * c) for c in range(4)]
+
+        def turn_and_round(i, c, bank):
+            for b in range(4):
+                nc.tensor.transpose(bank[:, P * b : P * (b + 1)], pages[i][:, N * c + P * b : N * c + P * (b + 1)], identity[:])
+            nc.scalar.copy(
+                turned[c][:, :, :, 32 * i : 32 * (i + 1), :],
+                bank[:].rearrange("t (b p u e) -> t b u p e", b=4, u=2, e=2),
             )
 
-        halves = [slice(0, N), slice(N, S)]
-        first_product(0, 0)
-        first_product(1, 0)
-        scatter(0, halves[0])
-        handq.append(quantize(group_hand(hand_raw[1][:], "hand_g1"), "hand1"))
-        scatter(1, halves[0])
-        first_product(0, 1)
-        first_product(1, 1)
-        wh_g1 = group_wh(wh_raw[1], rotating([P, 4 * N], BF16, "grouped", 4, "wh_g1"))
-        turn_wgs()
-        for h in (1, 0):
-            for i in (2, 3):
-                first_product(i, h)
-        for i in (2, 3):
-            repeat_rows(i)
-            make_weights(i)
-        scatter(0, halves[1])
-        w4.append(permute_w4(1, rotating([P, 2, 2 * N], U8, "act0", 1, "w4_1")))
-        scatter(1, halves[1])
-        whq.append(quantize(wh_g1, "wh1", rotating([P, N], U32, "act1", 1, "wh1_codes")))
-        first_pairs = placed.tile([P, 2, T, 2], BF16, name="first_pairs", offset=16384, align_bytes=64)
+        def turn_back(c):
+            grouped = place([P, 4 * N], BF16, f"page_g0{c}", GROUPED_AT + 4 * KB * c)
+            words = turned[c][:].rearrange("t b u p e -> t (b u p e)").bitcast(F32)
+            for half in range(2):
+                bank = banks[(2 * c + half) % 4]
+                for u in range(2):
+                    for b in range(2):
+                        at = P * (2 * (2 * half + b) + u)
+                        nc.tensor.transpose(bank[:, P * (2 * u + b) : P * (2 * u + b + 1)], words[:, at : at + P], identity[:])
+                nc.scalar.copy(
+                    grouped[:, 2 * N * half : 2 * N * (half + 1)].bitcast(F32).rearrange("p (t u) -> p t u", u=2),
+                    bank[:].rearrange("p (u t) -> p t u", u=2),
+                )
+            return grouped
 
-        def round_first(i):
-            nc.scalar.copy(first_pairs[:, i // 2, :, i % 2], pages[i][:])
-            if i + 5 < 8:
-                pages.append(load_page(i + 5))
+        def turned_product(block):
+            bank = banks[4 + len(sums) % 4]
+            sums.append((4, block))
+            at = P * block
+            for k in range(2):
+                nc.tensor.matmul_mx(
+                    out=bank[:], lhsT=v[k][at // N][:, at % N : at % N + P].bitcast(FP8X4), lhsT_scale=v_plane[k][:, at : at + P],
+                    rhs=w4[1][:, k, 2 * (N - 256) : 2 * (H - 256)].bitcast(FP4X4), rhs_scale=w4_planes[:, k, N:H], start=(k == 0), stop=False,
+                )
+            codes, scales = handq[at // QUARTER]
+            nc.tensor.matmul_mx(
+                out=bank[:], lhsT=codes[:, at % QUARTER : at % QUARTER + P].bitcast(FP8X4), lhsT_scale=scales[:, at % QUARTER : at % QUARTER + P],
+                rhs=whq[2][0][:].bitcast(FP8X4), rhs_scale=whq[2][1][:], start=False, stop=True,
+            )
+            gelus = place([P, 4, P], F32, f"gelus{block}", TURNED_AT + 2 * KB * block)
+            nc.scalar.activation(gelus[:], bank[:].rearrange("j (p t) -> j t p", t=4), GELU)
+            return gelus
+
+        def dealt_tile(i):
+            t = i - 4
+            acts[i, 0] = place([P, S], F32, f"act{i}", ACT_AT + 4 * KB * t)
+            for h in range(2):
+                bank = banks[2 * (t % 2) + h]
+                for b in range(4):
+                    nc.tensor.transpose(bank[:, P * b : P * (b + 1)], turned_gelus[4 * h + b][:, t, :], identity[:])
+                nc.scalar.activation(acts[i, 0][:, N * h : N * (h + 1)], bank[:], COPY, scale=dealt_gains[:, t : t + 1])
 
         def round_into_pairs(i, c):
-            t = i % 4
-            nc.scalar.copy(pairs[c][:, t // 2, :, t % 2], pages[i][:, c * N : (c + 1) * N])
+            t = i - 4
+            nc.scalar.copy(pairs[c][:, t // 2, :, t % 2], pages[i][:, N * c : N * (c + 1)])
 
-        round_first(0)
-        for h in range(2):
-            first_product(4, h)
-        make_weights(4)
-        round_first(1)
-        scatter(2, slice(0, S))
-        for i in range(5, 8):
-            for h in range(2):
-                first_product(i, h)
-            make_weights(i)
-        round_first(2)
-        scatter(3, slice(0, S))
-        v2_plane = rotating([P, S2], U8, "act3", 1, "v2_plane")
-        nc.vector.tensor_copy(v2_plane[:], tab2_plane[:].indirect(idx2[:]))
-        round_first(3)
-        woven = [weave(nc.scalar.copy, first_pairs[:, :, c * N : (c + 1) * N, :], f"page_g0{c}") for c in range(4)]
-        pairs = [rotating([P, 2, N, 2], BF16, "pairs", 4, f"pairs{c}") for c in range(4)]
-        for i in range(4, 8):
-            scatter(i, slice(0, S))
-            if i < 7:
-                for c in range(4):
-                    round_into_pairs(i, c)
-        pageq = [[], []]
-        cap_rows = placed.tile([P, 4, S], F32, name="cap_rows", offset=16384, align_bytes=64)
+        def weave(copy, c):
+            grouped = place([P, 4 * N], BF16, f"page_g1{c}", TURNED_AT + 4 * KB * c)
+            copy(
+                grouped[:].bitcast(F32).rearrange("p (c u) -> p c u", u=2),
+                pairs[c][:].rearrange("p u c e -> p u (c e)").bitcast(F32).rearrange("p u c -> p c u"),
+            )
+            return grouped
+
+        gather_v(0, 0)
+        for k in range(2):
+            nc.vector.tensor_copy(v_plane[k][:], tab_planes[:, k, :].indirect(idx[:]))
+        whq = [quantize(group_wh(0, GROUPED_AT + 8 * KB), "wh0")]
+        handq = [quantize(group_hand(q), f"hand{q}") for q in range(2)]
+        gather_v(0, 1)
+        gather_v(1, 0)
+        gather_v(1, 1)
+        make_weights(0, 0, N, HAND_AT + 4 * KB)
+        part_tile(0, 0, N, ACT_AT)
+        make_weights(1, 0, N, HAND_AT + 6 * KB)
+        hand_g2 = group_hand(2)
+        part_tile(1, 0, N, HAND_AT + 8 * KB)
+        scatter(0, 0, N)
+        handq.append(quantize(hand_g2, "hand2"))
+        scatter(1, 0, N)
+        handq.append(quantize(group_hand(3), "hand3"))
+        make_weights(0, 512, 768, HAND_AT + 12 * KB)
+        part_tile(0, 512, 768, HAND_AT + 13 * KB)
+        turn_gains(2, 4, banks[5])
+        wh_g1 = group_wh(1, GROUPED_AT + 6 * KB)
+        make_weights(0, 768, S, HAND_AT + 14 * KB)
+        part_tile(0, 768, S, ACT_AT + 2 * KB)
+        make_weights(1, N, S, HAND_AT + 15 * KB)
+        part_tile(1, N, S, ACT_AT + 6 * KB)
+        scatter(0, 512, 768)
+        whq.append(quantize(wh_g1, "wh1"))
+        scatter(0, 768, S)
+        wh_g2 = group_wh(2, GROUPED_AT + 12 * KB)
+        scatter(1, N, S)
+        whq.append(quantize(wh_g2, "wh2"))
+        for i in (2, 3):
+            whole_tile(i)
+        turned_gelus = [turned_product(block) for block in range(8)]
+
+        for i in range(4):
+            if i >= 1:
+                scatter(i + 1, 0, S)
+            dealt_tile(i + 4)
+            for c in range(4):
+                turn_and_round(i, c, banks[2 * (i % 2) + c % 2])
+            if i in (1, 2):
+                load_dealt_wgs(i + 5)
+                pages.append(load_page(i + 5))
+        tab2 = [load_table_words(tab2_words, a, f"tab2_{a}") for a in range(2)]
+        cap_rows = place([P, 4, S], F32, "cap_rows", WH_AT)
         nc.sync.dma_start(cap_rows[:], cap.rearrange("(n p) m -> p n m", n=4))
-        caps = [cap_rows[:, n, :] for n in range(4)]
+        woven = [turn_back(c) for c in range(4)]
+        pairs = [place([P, 2, N, 2], BF16, f"pairs{c}", HAND_AT + 4 * KB * c) for c in range(4)]
+        for i in range(4, 7):
+            scatter(i + 1, 0, S)
+            for c in range(4):
+                round_into_pairs(i, c)
 
-        scores = [rotating([P, T], F32, "page", 5, f"scores{n}") for n in range(4)]
-        for c in range(4):
-            round_into_pairs(7, c)
-        v2 = [rotating([P, 2, S2 // 2], U32, "act7", 1, "v2_0")]
+        last_act = ACT_AT + 4 * KB * 3
+        last_weights = WEIGHTS_AT + 4 * KB * 3
+        v2_plane = place([P, S2], U8, "v2_plane", last_act + 2 * KB)
+        nc.vector.tensor_copy(v2_plane[:], tab2_plane[:].indirect(idx2[:]))
+        v2 = [place([P, 2, S2 // 2], U32, "v2_0", last_weights)]
 
         def gather_v2(u, a):
             nc.vector.tensor_copy(v2[u][:, a, :], tab2[a][:].indirect(idx2[:, 16 * u : 16 * u + 16]))
 
-        gather_v2(0, 0)
-        first_codes = rotating([P, 4, N], U32, "last_weights", 1, "page0_codes")
+        def second_product(n, c):
+            for a in range(2):
+                nc.tensor.matmul_mx(
+                    out=banks[4 * (n % 2) + c][:], lhsT=v2[n // 2][:, a, P * (n % 2) : P * (n % 2 + 1)].bitcast(FP8X4),
+                    lhsT_scale=v2_plane[4 * a : P, P * n : P * (n + 1)],
+                    rhs=pageq[a][c][0][:].bitcast(FP8X4), rhs_scale=pageq[a][c][1][:], start=(a == 0), stop=(a == 1),
+                )
 
-        def quantize_and_multiply(a, c, grouped, codes=None):
-            pageq[a].append(quantize(grouped, f"page{a}{c}", codes))
-            for n in range(2):
-                second_product(n, c, a)
-
-        last = []
-        for c in range(2):
-            quantize_and_multiply(0, c, woven[c], first_codes[:, c, :])
-            last.append(weave(nc.vector.tensor_copy, pairs[c][:], f"page_g1{c}"))
-        gather_v2(0, 1)
-        for c in range(2, 4):
-            last.append(weave(nc.scalar.copy, pairs[c][:], f"page_g1{c}", ("act4", "act1")[c - 2], 1))
-        for c in range(2):
-            quantize_and_multiply(1, c, last[c])
-            quantize_and_multiply(0, c + 2, woven[c + 2], first_codes[:, c + 2, :])
-        for c in range(2, 4):
-            quantize_and_multiply(1, c, last[c])
-        v2.append(rotating([P, 2, S2 // 2], U32, "act1", 1, "v2_1"))
+        for a in range(2):
+            gather_v2(0, a)
+        for c in range(4):
+            round_into_pairs(7, c)
+        last = [weave(nc.vector.tensor_copy if c == 0 else nc.scalar.copy, c) for c in range(4)]
+        pageq = [[quantize(woven[c], f"page0{c}", place([P, N], U8, f"page0{c}_scales", last_act + N * c)) for c in range(4)], []]
+        for c in range(4):
+            pageq[1].append(quantize(last[c], f"page1{c}"))
+        v2.append(place([P, 2, S2 // 2], U32, "v2_1", TURNED_AT + 12 * KB))
         for a in range(2):
             gather_v2(1, a)
 
+        scores = [place([P, T], F32, f"scores{n}", PAGE_AT + 8 * KB * n) for n in range(4)]
+
         def cap_and_store(n, cols, picked):
-            nc.vector.tensor_tensor(picked[:], picked[:], caps[n][:, cols], MIN)
+            nc.vector.tensor_tensor(picked[:], picked[:], cap_rows[:, n, cols], MIN)
             nc.sync.dma_start(out[P * n : P * (n + 1), cols], picked[:])
 
         waiting = []
         for n in range(4):
             for c in range(4):
-                if n >= 2:
-                    for a in range(2):
-                        second_product(n, c, a)
-                nc.scalar.copy(scores[n][:, c * N : (c + 1) * N], banks[4 * ((n + 1) % 2) + c][:])
+                second_product(n, c)
+                nc.scalar.copy(scores[n][:, c * N : (c + 1) * N], banks[4 * (n % 2) + c][:])
             edges = [0, 512, 768, S] if n == 3 else [0, S]
             for lo, hi in zip(edges[:-1], edges[1:]):
-                picked = rotating([P, hi - lo], F32, "picked", 4, f"picked{n}_{lo}")
+                picked = place([P, hi - lo], F32, f"picked{n}_{lo}", PAGE_AT + 8 * KB * (4 + n) + 4 * lo)
                 nc.vector.tensor_copy(picked[:], scores[n][:].indirect(idx4[:, lo // 16 : hi // 16]))
                 waiting.append((n, slice(lo, hi), picked))
                 if len(waiting) == 2:

@@ -186,8 +186,8 @@ def tile_list_drop_move_adviser_kernel(
         v = [[keep([P, N], U32, "v00"), keep([P, N], U32, "v01")], [keep([P, N], U32, "v10"), keep([P, N], U32, "v11")]]
         v_plane = [keep([P, S], U8, f"v_plane{k}") for k in range(2)]
 
-        def gather_v(k, h):
-            nc.vector.tensor_copy(v[k][h][:], tab[k][:].indirect(idx[:, 32 * h : 32 * (h + 1)]))
+        def gather_v(k, lo, hi):
+            nc.vector.tensor_copy(v[k][lo // N][:, lo % N : lo % N + hi - lo], tab[k][:].indirect(idx[:, lo // 16 : hi // 16]))
 
         def group_wh(n, offset):
             return group(wh_raw[n], f"wh_g{n}", offset)
@@ -206,8 +206,7 @@ def tile_list_drop_move_adviser_kernel(
 
         def first_product(i, lo, hi, act):
             bank = banks[4 + len(sums) % 4]
-            if (i, lo) != (0, 0):
-                sums.append((i, lo))
+            sums.append((i, lo))
             n4 = piece(w4_edges, P * i)
             at4 = P * i - w4_edges[n4]
             nh = piece(wh_edges, P * i)
@@ -223,7 +222,8 @@ def tile_list_drop_move_adviser_kernel(
                  handq[at // QUARTER][0][:], handq[at // QUARTER][1][:])
                 for at in range(lo, hi, QUARTER)
             ]
-            passes = table_passes + hand_passes if (i, lo) != (0, 0) else table_passes[:1] + hand_passes + table_passes[1:]
+            half = len(table_passes) // 2
+            passes = table_passes[:half] + hand_passes + table_passes[half:] if hi <= N and i < 2 else table_passes + hand_passes
             for step, (at, cols, lhsT, lhsT_scale, rhs, rhs_scale) in enumerate(passes):
                 nc.tensor.matmul_mx(
                     out=bank[:, at - lo : at - lo + cols], lhsT=lhsT, lhsT_scale=lhsT_scale, rhs=rhs.bitcast(FP8X4), rhs_scale=rhs_scale,
@@ -308,26 +308,28 @@ def tile_list_drop_move_adviser_kernel(
             )
             return grouped
 
-        gather_v(0, 0)
+        gather_v(0, 0, N)
         for k in range(2):
             nc.vector.tensor_copy(v_plane[k][:], tab_planes[:, k, :].indirect(idx[:]))
         whq = [quantize(group_wh(0, GROUPED_AT + 8 * KB), "wh0")]
         handq = [quantize(group_hand(q), f"hand{q}") for q in range(2)]
-        gather_v(0, 1)
-        gather_v(1, 0)
-        gather_v(1, 1)
+        gather_v(0, N, S)
+        for lo, hi in ((0, QUARTER), (QUARTER, N), (N, S)):
+            gather_v(1, lo, hi)
         make_weights(0, 0, N, HAND_AT + 4 * KB)
-        part_tile(0, 0, N, ACT_AT)
+        acts[0, 0] = place([P, N], F32, "act0_0", ACT_AT)
+        for lo in (0, QUARTER):
+            first_product(0, lo, lo + QUARTER, acts[0, 0][:, lo : lo + QUARTER])
         make_weights(1, 0, N, HAND_AT + 6 * KB)
+        part_tile(1, 0, N, ACT_AT + 4 * KB)
         hand_g2 = group_hand(2)
-        part_tile(1, 0, N, HAND_AT + 8 * KB)
         scatter(0, 0, N)
         handq.append(quantize(hand_g2, "hand2"))
         scatter(1, 0, N)
         handq.append(quantize(group_hand(3), "hand3"))
         make_weights(0, 512, 768, HAND_AT + 12 * KB)
         part_tile(0, 512, 768, HAND_AT + 13 * KB)
-        turn_gains(2, 4, banks[5])
+        turn_gains(2, 4, banks[7])
         wh_g1 = group_wh(1, GROUPED_AT + 6 * KB)
         make_weights(0, 768, S, HAND_AT + 14 * KB)
         part_tile(0, 768, S, ACT_AT + 2 * KB)

@@ -26,13 +26,13 @@ QUARTER = 256
 KB = 1024
 FLOPS = 5368709120
 
-TABLE_AT = 0
+TABLE_AT = 96 * KB
 HAND_AT = 16 * KB
 WH_AT = 32 * KB
 GROUPED_AT = 48 * KB
 TURNED_AT = 64 * KB
 ACT_AT = 80 * KB
-WEIGHTS_AT = 96 * KB
+WEIGHTS_AT = 0
 PAGE_AT = 112 * KB
 
 
@@ -90,9 +90,9 @@ def tile_list_drop_move_adviser_kernel(
             nc.sync.dma_start(tile[:], rows)
             return tile
 
-        def group(raw, name, offset):
+        def group(raw, name, offset, copy=nc.scalar.copy):
             grouped = place([P, 4 * raw.shape[2]], BF16, name, offset)
-            nc.scalar.copy(
+            copy(
                 grouped[:].rearrange("p (c i j) -> p c j i", i=4, j=4),
                 raw[:].rearrange("p j (c i) -> p c j i", i=4),
             )
@@ -112,19 +112,23 @@ def tile_list_drop_move_adviser_kernel(
         def piece(edges, col):
             return max(n for n in range(len(edges) - 1) if edges[n] <= col)
 
-        tab_planes = keep([P, 2, T], U8, "tab_planes")
+        tab_rows = place([P, T], U8, "tab_rows", PAGE_AT - KB)
+        v_planes = keep([P, 2, S], U8, "v_planes")
+        v_plane = [v_planes[:, k, :] for k in range(2)]
         w4_planes = keep([P, 2, H], U8, "w4_planes")
         tab2_plane = keep([P, T], U8, "tab2_plane")
         gain_rows = keep([P, P], F32, "gain_rows")
-        nc.vector.memset(tab_planes[:].bitcast(I32), 0)
-        nc.vector.memset(w4_planes[:].bitcast(I32), 0)
         nc.vector.memset(gain_rows[:], 0.0)
+        nc.vector.memset(w4_planes[:].bitcast(I32), 0)
+        nc.vector.memset(tab_rows[32:64, :].bitcast(I32), 0)
+        nc.vector.memset(tab_rows[64:P, :].bitcast(I32), 0)
+        nc.vector.memset(v_planes[:].bitcast(I32), 0)
         nc.vector.memset(tab2_plane[:].bitcast(I32), 0)
+        table_warm_up = keep([P, 1], F32, "table_warm_up")
+        nc.scalar.activation(table_warm_up[:], gain_rows[:, 0:1], GELU)
         identity = keep([P, P], F32, "identity")
         make_identity(nc, identity[:])
 
-        table_warm_up = keep([P, 1], F32, "table_warm_up")
-        nc.scalar.activation(table_warm_up[:], identity[:, 0:1], GELU)
 
         def load_wgs(h):
             rows = keep([P, N], F32, f"wgs{h}")
@@ -135,16 +139,26 @@ def tile_list_drop_move_adviser_kernel(
             return load_rows(hand, QUARTER * q, QUARTER * (q + 1), HAND_AT + 4 * KB * q, f"hand_raw{q}")
 
         idx = load_list(offs, "idx")
+        nc.sync.dma_start(tab_rows[0:32, :].bitcast(I32), tab_scales.rearrange("a q n -> q a n").bitcast(I32))
         tab = [load_table_words(tab_words, 0, "tab0")]
         w4 = [load_w4(0, 256)]
         idx3 = load_list(offs3, "idx3")
-        load_planes_side_by_side(tab_scales, tab_planes)
-        nc.sync.dma_start(gain_rows[0:4, :], gain[0:N].rearrange("(c m) -> c m", m=P))
-        wh_raw = [load_rows(wh, 0, 256, WH_AT, "wh_raw0")]
-        hand_raw = [load_hand(0), load_hand(1)]
-        tab.append(load_table_words(tab_words, 1, "tab1"))
         load_planes_side_by_side(w4_scales, w4_planes)
+        hand_raw = [load_rows(hand, 0, N, HAND_AT, "hand_raw0"), None]
+        wh_raw = [load_rows(wh, 0, 256, WH_AT, "wh_raw0")]
+        nc.sync.dma_start(gain_rows[0:4, :], gain[0:N].rearrange("(c m) -> c m", m=P))
+        v_rows = keep([P, S], U8, "v_rows")
+        nc.vector.tensor_copy(v_rows[:], tab_rows[:].indirect(idx[:]))
+        for q in (0, 2, 1, 3):
+            nc.sync.dma_start(v_planes[32 * q : 32 * q + 4, :, :].bitcast(I32), v_rows[8 * q : 8 * q + 8, :].bitcast(I32))
+        tab.append(load_table_words(tab_words, 1, "tab1"))
         wgs_rows = [load_wgs(0)]
+        v = [[keep([P, N], U32, "v00"), keep([P, N], U32, "v01")], [keep([P, N], U32, "v10"), keep([P, N], U32, "v11")]]
+
+        def gather_v(k, lo, hi):
+            nc.vector.tensor_copy(v[k][lo // N][:, lo % N : lo % N + hi - lo], tab[k][:].indirect(idx[:, lo // 16 : hi // 16]))
+
+        gather_v(0, 0, N)
         pages = [load_page(0)]
         hand_raw.append(load_hand(2))
         pages.append(load_page(1))
@@ -181,13 +195,6 @@ def tile_list_drop_move_adviser_kernel(
             for i in range(lo, hi):
                 gains[i] = turned_gains[:, i - lo : i - lo + 1]
 
-        turn_gains(0, 2, banks[0])
-
-        v = [[keep([P, N], U32, "v00"), keep([P, N], U32, "v01")], [keep([P, N], U32, "v10"), keep([P, N], U32, "v11")]]
-        v_plane = [keep([P, S], U8, f"v_plane{k}") for k in range(2)]
-
-        def gather_v(k, lo, hi):
-            nc.vector.tensor_copy(v[k][lo // N][:, lo % N : lo % N + hi - lo], tab[k][:].indirect(idx[:, lo // 16 : hi // 16]))
 
         def group_wh(n, offset):
             return group(wh_raw[n], f"wh_g{n}", offset)
@@ -205,25 +212,24 @@ def tile_list_drop_move_adviser_kernel(
                 nc.scalar.activation(weights[i, lo][:, first - lo : last - lo], wgs_rows[h][:, first - N * h : last - N * h], COPY, scale=gains[i])
 
         def first_product(i, lo, hi, act):
-            bank = banks[4 + len(sums) % 4]
+            bank = banks[4 + len(sums) % (3 if len(sums) < 6 else 4)]
             sums.append((i, lo))
             n4 = piece(w4_edges, P * i)
             at4 = P * i - w4_edges[n4]
             nh = piece(wh_edges, P * i)
             ath = P * i - wh_edges[nh]
-            width = N if hi - lo == N else P
+            width = hi - lo
             table_passes = [
-                (at, width, w4[n4][:, k, 2 * at4 : 2 * (at4 + P)].bitcast(FP4X4), w4_planes[:, k, P * i : P * (i + 1)],
-                 v[k][at // N][:, at % N : at % N + width], v_plane[k][:, at : at + width])
-                for k in range(2) for at in range(lo, hi, width)
+                (lo, width, w4[n4][:, k, 2 * at4 : 2 * (at4 + P)].bitcast(FP4X4), w4_planes[:, k, P * i : P * (i + 1)],
+                 v[k][lo // N][:, lo % N : lo % N + width], v_plane[k][:, lo:hi])
+                for k in range(2)
             ]
             hand_passes = [
-                (at, QUARTER, whq[nh][0][:, ath : ath + P].bitcast(FP8X4), whq[nh][1][:, ath : ath + P],
-                 handq[at // QUARTER][0][:], handq[at // QUARTER][1][:])
-                for at in range(lo, hi, QUARTER)
+                (max(lo, at), min(hi, end) - max(lo, at), whq[nh][0][:, ath : ath + P].bitcast(FP8X4), whq[nh][1][:, ath : ath + P],
+                 codes[:, max(lo, at) - at : min(hi, end) - at], scales[:, max(lo, at) - at : min(hi, end) - at])
+                for (at, end), (codes, scales) in handq.items() if max(lo, at) < min(hi, end)
             ]
-            half = len(table_passes) // 2
-            passes = table_passes[:half] + hand_passes + table_passes[half:] if hi <= N and i < 2 else table_passes + hand_passes
+            passes = table_passes[:1] + hand_passes + table_passes[1:] if hi <= N and i < 2 else table_passes + hand_passes
             for step, (at, cols, lhsT, lhsT_scale, rhs, rhs_scale) in enumerate(passes):
                 nc.tensor.matmul_mx(
                     out=bank[:, at - lo : at - lo + cols], lhsT=lhsT, lhsT_scale=lhsT_scale, rhs=rhs.bitcast(FP8X4), rhs_scale=rhs_scale,
@@ -278,9 +284,10 @@ def tile_list_drop_move_adviser_kernel(
                     out=bank[:], lhsT=v[k][at // N][:, at % N : at % N + P].bitcast(FP8X4), lhsT_scale=v_plane[k][:, at : at + P],
                     rhs=w4[1][:, k, 2 * (N - 256) : 2 * (H - 256)].bitcast(FP4X4), rhs_scale=w4_planes[:, k, N:H], start=(k == 0), stop=False,
                 )
-            codes, scales = handq[at // QUARTER]
+            begin, end = max(key for key in handq if key[0] <= at)
+            codes, scales = handq[begin, end]
             nc.tensor.matmul_mx(
-                out=bank[:], lhsT=codes[:, at % QUARTER : at % QUARTER + P].bitcast(FP8X4), lhsT_scale=scales[:, at % QUARTER : at % QUARTER + P],
+                out=bank[:], lhsT=codes[:, at - begin : at - begin + P].bitcast(FP8X4), lhsT_scale=scales[:, at - begin : at - begin + P],
                 rhs=whq[2][0][:].bitcast(FP8X4), rhs_scale=whq[2][1][:], start=False, stop=True,
             )
             gelus = place([P, 4, P], F32, f"gelus{block}", TURNED_AT + 2 * KB * block)
@@ -308,12 +315,11 @@ def tile_list_drop_move_adviser_kernel(
             )
             return grouped
 
-        gather_v(0, 0, N)
-        for k in range(2):
-            nc.vector.tensor_copy(v_plane[k][:], tab_planes[:, k, :].indirect(idx[:]))
-        whq = [quantize(group_wh(0, GROUPED_AT + 8 * KB), "wh0")]
-        handq = [quantize(group_hand(q), f"hand{q}") for q in range(2)]
         gather_v(0, N, S)
+        hand_g0 = group_hand(0)
+        turn_gains(0, 2, banks[0])
+        whq = [quantize(group(wh_raw[0], "wh_g0", GROUPED_AT + 8 * KB, nc.vector.tensor_copy), "wh0")]
+        handq = {(0, N): quantize(hand_g0, "hand0")}
         for lo, hi in ((0, QUARTER), (QUARTER, N), (N, S)):
             gather_v(1, lo, hi)
         make_weights(0, 0, N, HAND_AT + 4 * KB)
@@ -324,9 +330,9 @@ def tile_list_drop_move_adviser_kernel(
         part_tile(1, 0, N, ACT_AT + 4 * KB)
         hand_g2 = group_hand(2)
         scatter(0, 0, N)
-        handq.append(quantize(hand_g2, "hand2"))
+        handq[512, 768] = quantize(hand_g2, "hand2")
         scatter(1, 0, N)
-        handq.append(quantize(group_hand(3), "hand3"))
+        handq[768, S] = quantize(group_hand(3), "hand3")
         make_weights(0, 512, 768, HAND_AT + 12 * KB)
         part_tile(0, 512, 768, HAND_AT + 13 * KB)
         turn_gains(2, 4, banks[7])

@@ -13,6 +13,8 @@ FP8X4 = mybir.dt.float8_e4m3fn_x4
 FP4X4 = mybir.dt.float4_e2m1fn_x4
 MULT = mybir.AluOpType.mult
 MIN = mybir.AluOpType.min
+MAX = mybir.AluOpType.max
+SUB = mybir.AluOpType.subtract
 GELU = mybir.ActivationFunctionType.Gelu_apprx_tanh
 COPY = mybir.ActivationFunctionType.Copy
 
@@ -401,20 +403,36 @@ def tile_list_drop_move_adviser_kernel(
 
         scores = [place([P, T], F32, f"scores{n}", PAGE_AT + 8 * KB * n) for n in range(4)]
 
-        def cap_and_store(n, cols, picked):
-            nc.vector.tensor_tensor(picked[:], picked[:], cap_rows[:, n, cols], MIN)
-            nc.sync.dma_start(out[P * n : P * (n + 1), cols], picked[:])
-
-        waiting = []
-        for n in range(4):
+        def score(n):
             for c in range(4):
                 second_product(n, c)
                 nc.scalar.copy(scores[n][:, c * N : (c + 1) * N], banks[4 * (n % 2) + c][:])
-            edges = [0, 512, 768, S] if n == 3 else [0, S]
-            for lo, hi in zip(edges[:-1], edges[1:]):
-                picked = place([P, hi - lo], F32, f"picked{n}_{lo}", PAGE_AT + 8 * KB * (4 + n) + 4 * lo)
-                nc.vector.tensor_copy(picked[:], scores[n][:].indirect(idx4[:, lo // 16 : hi // 16]))
-                waiting.append((n, slice(lo, hi), picked))
-                if len(waiting) == 2:
-                    cap_and_store(*waiting.pop(0))
-        cap_and_store(*waiting.pop(0))
+
+        def pick(n, lo, hi):
+            picked = place([P, hi - lo], F32, f"picked{n}_{lo}", PAGE_AT + 8 * KB * (4 + n) if lo == 0 else ACT_AT + 4 * KB + 4 * lo)
+            nc.vector.tensor_copy(picked[:], scores[n][:].indirect(idx4[:, lo // 16 : hi // 16]))
+            return picked
+
+        def cap_and_store(n, lo, hi, picked, capped):
+            nc.vector.tensor_tensor(capped[:], picked[:], cap_rows[:, n, lo:hi], MIN)
+            nc.sync.dma_start(out[P * n : P * (n + 1), lo:hi], capped[:])
+
+        score(0)
+        first = pick(0, 0, S)
+        excess = place([P, S], F32, "excess", ACT_AT)
+        nc.gpsimd.tensor_tensor(excess[:], first[:], cap_rows[:, 0, :], SUB)
+        nc.gpsimd.tensor_scalar(excess[:], excess[:], float("inf"), 0.0, MIN, MAX)
+        nc.gpsimd.tensor_tensor(first[:], first[:], excess[:], SUB)
+        nc.sync.dma_start(out[0:P, :], first[:])
+        score(1)
+        second = pick(1, 0, S)
+        score(2)
+        third = pick(2, 0, S)
+        score(3)
+        cap_and_store(3, 0, N, pick(3, 0, N), place([P, N], F32, "capped3", ACT_AT))
+        cap_and_store(1, 0, S, second, place([P, S], F32, "capped1", PAGE_AT + 53 * KB))
+        next_to_last = pick(3, 512, 768)
+        cap_and_store(2, 0, S, third, place([P, S], F32, "capped2", PAGE_AT + 57 * KB))
+        very_last = pick(3, 768, S)
+        cap_and_store(3, 512, 768, next_to_last, next_to_last)
+        cap_and_store(3, 768, S, very_last, very_last)

from contextlib import ExitStack

import concourse.mybir as mybir
from concourse.masks import make_identity

F32 = mybir.dt.float32
BF16 = mybir.dt.bfloat16
I32 = mybir.dt.int32
U32 = mybir.dt.uint32
U16 = mybir.dt.uint16
U8 = mybir.dt.uint8
FP8X4 = mybir.dt.float8_e4m3fn_x4
FP4X4 = mybir.dt.float4_e2m1fn_x4
MULT = mybir.AluOpType.mult
MIN = mybir.AluOpType.min
MAX = mybir.AluOpType.max
SUB = mybir.AluOpType.subtract
GELU = mybir.ActivationFunctionType.Gelu_apprx_tanh
COPY = mybir.ActivationFunctionType.Copy

P = 128
T = 2048
S = 1024
S2 = 512
H = 1024
N = 512
QUARTER = 256
KB = 1024
FLOPS = 5368709120

TABLE_AT = 96 * KB
HAND_AT = 16 * KB
WH_AT = 32 * KB
GROUPED_AT = 48 * KB
TURNED_AT = 64 * KB
ACT_AT = 80 * KB
WEIGHTS_AT = 0
PAGE_AT = 112 * KB


def tile_list_drop_move_adviser_kernel(
    tc, tab_words, tab_scales, offs, w4_words, w4_scales, hand, wh, gain, page0, wgs, offs3,
    tab2_words, tab2_scales, offs2, offs4, cap, out,
):
    nc = tc.nc
    with ExitStack() as ctx:
        held = ctx.enter_context(tc.tile_pool(name="held", bufs=1))
        placed = ctx.enter_context(tc.tile_pool(name="placed", bufs=1))
        psum = ctx.enter_context(tc.psum_pool(name="psum", bufs=1))
        banks = [psum.tile([P, N], F32, name=f"bank{b}") for b in range(8)]

        def keep(shape, dtype, name):
            return held.tile(shape, dtype, name=name, align_bytes=64)

        def place(shape, dtype, name, offset):
            return placed.tile(shape, dtype, name=name, offset=offset, align_bytes=64)

        def load_list(src, name):
            lst = held.tile(list(src.shape), U16, name=name)
            nc.sync.dma_start(lst[:], src)
            return lst

        def load_planes_side_by_side(src, planes):
            for q in (0, 2, 1, 3):
                nc.sync.dma_start(
                    planes[32 * q : 32 * q + 4, :, :].bitcast(I32),
                    src[:, 4 * q : 4 * q + 4, :].rearrange("k r n -> r k n").bitcast(I32),
                )

        def load_planes_stacked(src, plane):
            for q in range(4):
                nc.sync.dma_start(plane[32 * q : 32 * q + 8, :].bitcast(I32), src[:, 4 * q : 4 * q + 4, :].bitcast(I32))

        def load_table_words(src, a, name):
            words = place([P, T], U32, name, TABLE_AT + 8 * KB * a)
            nc.sync.dma_start(words[:].bitcast(I32), src[a].rearrange("p t i -> p (t i)").bitcast(I32))
            return words

        def load_w4(lo, hi):
            words = keep([P, 2, 2 * (hi - lo)], U8, f"w4_{lo}")
            nc.sync.dma_start(words[:].bitcast(I32), w4_words[:, :, 2 * lo : 2 * hi].rearrange("k p b -> p k b").bitcast(I32))
            return words

        def load_rows(src, lo, hi, offset, name):
            raw = place([P, 4, hi - lo], F32, name, offset)
            nc.sync.dma_start(raw[:], src[:, lo:hi].rearrange("(p j) c -> p j c", j=4))
            return raw

        def load_page(i):
            tile = place([P, T], F32, f"page{i}", PAGE_AT + 8 * KB * i)
            rows = page0[P * i : P * (i + 1), :] if i < 4 else page0[N:H, :].rearrange("(p t) c -> t p c", t=4)[i - 4]
            nc.sync.dma_start(tile[:], rows)
            return tile

        def group(raw, name, offset, copy=nc.scalar.copy):
            grouped = place([P, 4 * raw.shape[2]], BF16, name, offset)
            copy(
                grouped[:].rearrange("p (c i j) -> p c j i", i=4, j=4),
                raw[:].rearrange("p j (c i) -> p c j i", i=4),
            )
            return grouped

        def quantize(grouped, name, scales=None):
            width = grouped.shape[1] // 4
            codes = keep([P, width], U32, name + "_codes")
            if scales is None:
                scales = keep([P, width], U8, name + "_scales")
            nc.vector.quantize_mx(out=codes[:].bitcast(FP8X4), scales=scales[:], in_=grouped[:])
            return codes, scales

        wh_edges = [0, 256, 512, H]
        w4_edges = [0, 256, H]

        def piece(edges, col):
            return max(n for n in range(len(edges) - 1) if edges[n] <= col)

        tab_rows = place([P, T], U8, "tab_rows", PAGE_AT - KB)
        v_planes = keep([P, 2, S], U8, "v_planes")
        v_plane = [v_planes[:, k, :] for k in range(2)]
        w4_planes = keep([P, 2, H], U8, "w4_planes")
        tab2_plane = keep([P, T], U8, "tab2_plane")
        gain_rows = keep([P, P], F32, "gain_rows")
        nc.vector.memset(gain_rows[:], 0.0)
        nc.vector.memset(w4_planes[:].bitcast(I32), 0)
        nc.vector.memset(tab_rows[32:64, :].bitcast(I32), 0)
        nc.vector.memset(tab_rows[64:P, :].bitcast(I32), 0)
        nc.vector.memset(v_planes[:].bitcast(I32), 0)
        nc.vector.memset(tab2_plane[:].bitcast(I32), 0)
        table_warm_up = keep([P, 1], F32, "table_warm_up")
        nc.scalar.activation(table_warm_up[:], gain_rows[:, 0:1], GELU)
        identity = keep([P, P], F32, "identity")
        make_identity(nc, identity[:])


        def load_wgs(h):
            rows = keep([P, N], F32, f"wgs{h}")
            nc.sync.dma_start(rows[:], wgs[:, N * h : N * (h + 1)])
            return rows

        def load_hand(q):
            return load_rows(hand, QUARTER * q, QUARTER * (q + 1), HAND_AT + 4 * KB * q, f"hand_raw{q}")

        idx = load_list(offs, "idx")
        nc.sync.dma_start(tab_rows[0:32, :].bitcast(I32), tab_scales.rearrange("a q n -> q a n").bitcast(I32))
        tab = [load_table_words(tab_words, 0, "tab0")]
        w4 = [load_w4(0, 256)]
        idx3 = load_list(offs3, "idx3")
        load_planes_side_by_side(w4_scales, w4_planes)
        hand_raw = [load_rows(hand, 0, N, HAND_AT, "hand_raw0"), None]
        wh_raw = [load_rows(wh, 0, 256, WH_AT, "wh_raw0")]
        nc.sync.dma_start(gain_rows[0:4, :], gain[0:N].rearrange("(c m) -> c m", m=P))
        v_rows = keep([P, S], U8, "v_rows")
        nc.vector.tensor_copy(v_rows[:], tab_rows[:].indirect(idx[:]))
        for q in (0, 2, 1, 3):
            nc.sync.dma_start(v_planes[32 * q : 32 * q + 4, :, :].bitcast(I32), v_rows[8 * q : 8 * q + 8, :].bitcast(I32))
        tab.append(load_table_words(tab_words, 1, "tab1"))
        wgs_rows = [load_wgs(0)]
        v = [[keep([P, N], U32, "v00"), keep([P, N], U32, "v01")], [keep([P, N], U32, "v10"), keep([P, N], U32, "v11")]]

        def gather_v(k, lo, hi):
            nc.vector.tensor_copy(v[k][lo // N][:, lo % N : lo % N + hi - lo], tab[k][:].indirect(idx[:, lo // 16 : hi // 16]))

        gather_v(0, 0, N)
        pages = [load_page(0)]
        hand_raw.append(load_hand(2))
        pages.append(load_page(1))
        hand_raw.append(load_hand(3))
        wgs_rows.append(load_wgs(1))
        wh_raw.append(load_rows(wh, 256, 512, WH_AT + 4 * KB, "wh_raw1"))
        wh_raw.append(load_rows(wh, 512, H, WH_AT + 8 * KB, "wh_raw2"))
        w4.append(load_w4(256, H))
        pages.append(load_page(2))
        pages.append(load_page(3))
        pages.append(load_page(4))
        idx2 = load_list(offs2, "idx2")
        idx4 = load_list(offs4, "idx4")
        dealt_gains = keep([P, 4], F32, "dealt_gains")
        nc.sync.dma_start(dealt_gains[:], gain[N:H].rearrange("(p t) -> p t", t=4))
        weights = {}

        def load_dealt_wgs(i):
            weights[i, 0] = place([P, S], F32, f"weights{i}", WEIGHTS_AT + 4 * KB * (i % 4))
            for q in range(4):
                nc.sync.dma_start(weights[i, 0][32 * q : 32 * (q + 1), :], wgs.rearrange("(m t) c -> t m c", t=4)[i - 4])

        load_dealt_wgs(4)
        load_dealt_wgs(5)
        load_planes_stacked(tab2_scales, tab2_plane)
        pages.append(load_page(5))

        gains = {}

        def turn_gains(lo, hi, bank):
            nc.tensor.transpose(bank[:, 0:P], gain_rows[:], identity[:])
            turned_gains = keep([P, hi - lo], F32, f"gains{lo}")
            nc.scalar.copy(turned_gains[:], bank[:, lo:hi])
            for i in range(lo, hi):
                gains[i] = turned_gains[:, i - lo : i - lo + 1]


        def group_wh(n, offset):
            return group(wh_raw[n], f"wh_g{n}", offset)

        def group_hand(q):
            return group(hand_raw[q], f"hand_g{q}", GROUPED_AT + 2 * KB * q)

        acts = {}
        sums = []

        def make_weights(i, lo, hi, offset):
            weights[i, lo] = place([P, hi - lo], F32, f"weights{i}_{lo}", offset)
            for h in range(lo // N, (hi - 1) // N + 1):
                first, last = max(lo, N * h), min(hi, N * (h + 1))
                nc.scalar.activation(weights[i, lo][:, first - lo : last - lo], wgs_rows[h][:, first - N * h : last - N * h], COPY, scale=gains[i])

        def first_product(i, lo, hi, act):
            bank = banks[4 + len(sums) % (3 if len(sums) < 6 else 4)]
            sums.append((i, lo))
            n4 = piece(w4_edges, P * i)
            at4 = P * i - w4_edges[n4]
            nh = piece(wh_edges, P * i)
            ath = P * i - wh_edges[nh]
            width = hi - lo
            table_passes = [
                (lo, width, w4[n4][:, k, 2 * at4 : 2 * (at4 + P)].bitcast(FP4X4), w4_planes[:, k, P * i : P * (i + 1)],
                 v[k][lo // N][:, lo % N : lo % N + width], v_plane[k][:, lo:hi])
                for k in range(2)
            ]
            hand_passes = [
                (max(lo, at), min(hi, end) - max(lo, at), whq[nh][0][:, ath : ath + P].bitcast(FP8X4), whq[nh][1][:, ath : ath + P],
                 codes[:, max(lo, at) - at : min(hi, end) - at], scales[:, max(lo, at) - at : min(hi, end) - at])
                for (at, end), (codes, scales) in handq.items() if max(lo, at) < min(hi, end)
            ]
            passes = table_passes[:1] + hand_passes + table_passes[1:] if hi <= N and i < 2 else table_passes + hand_passes
            for step, (at, cols, lhsT, lhsT_scale, rhs, rhs_scale) in enumerate(passes):
                nc.tensor.matmul_mx(
                    out=bank[:, at - lo : at - lo + cols], lhsT=lhsT, lhsT_scale=lhsT_scale, rhs=rhs.bitcast(FP8X4), rhs_scale=rhs_scale,
                    start=(step == 0), stop=(step == len(passes) - 1),
                )
            nc.scalar.activation(act, bank[:, 0 : hi - lo], GELU)

        def whole_tile(i):
            make_weights(i, 0, S, WEIGHTS_AT + 4 * KB * (i % 4))
            acts[i, 0] = place([P, S], F32, f"act{i}", ACT_AT + 4 * KB * (i % 4))
            for h in range(2):
                first_product(i, N * h, N * (h + 1), acts[i, 0][:, h * N : (h + 1) * N])

        def part_tile(i, lo, hi, offset):
            acts[i, lo] = place([P, hi - lo], F32, f"act{i}_{lo}", offset)
            first_product(i, lo, hi, acts[i, lo][:])

        def scatter(i, lo, hi):
            nc.vector.tensor_tensor(pages[i][:].indirect(idx3[:, lo // 16 : hi // 16]), acts[i, lo][:], weights[i, lo][:], MULT)

        turned = [place([P, 4, 2, P, 2], BF16, f"turned{c}", HAND_AT + 4 * KB * c) for c in range(4)]

        def turn_and_round(i, c, bank):
            for b in range(4):
                nc.tensor.transpose(bank[:, P * b : P * (b + 1)], pages[i][:, N * c + P * b : N * c + P * (b + 1)], identity[:])
            nc.scalar.copy(
                turned[c][:, :, :, 32 * i : 32 * (i + 1), :],
                bank[:].rearrange("t (b p u e) -> t b u p e", b=4, u=2, e=2),
            )

        def turn_back(c):
            grouped = place([P, 4 * N], BF16, f"page_g0{c}", GROUPED_AT + 4 * KB * c)
            words = turned[c][:].rearrange("t b u p e -> t (b u p e)").bitcast(F32)
            for half in range(2):
                bank = banks[(2 * c + half) % 4]
                for u in range(2):
                    for b in range(2):
                        at = P * (2 * (2 * half + b) + u)
                        nc.tensor.transpose(bank[:, P * (2 * u + b) : P * (2 * u + b + 1)], words[:, at : at + P], identity[:])
                nc.scalar.copy(
                    grouped[:, 2 * N * half : 2 * N * (half + 1)].bitcast(F32).rearrange("p (t u) -> p t u", u=2),
                    bank[:].rearrange("p (u t) -> p t u", u=2),
                )
            return grouped

        def turned_product(block):
            bank = banks[4 + len(sums) % 4]
            sums.append((4, block))
            at = P * block
            for k in range(2):
                nc.tensor.matmul_mx(
                    out=bank[:], lhsT=v[k][at // N][:, at % N : at % N + P].bitcast(FP8X4), lhsT_scale=v_plane[k][:, at : at + P],
                    rhs=w4[1][:, k, 2 * (N - 256) : 2 * (H - 256)].bitcast(FP4X4), rhs_scale=w4_planes[:, k, N:H], start=(k == 0), stop=False,
                )
            begin, end = max(key for key in handq if key[0] <= at)
            codes, scales = handq[begin, end]
            nc.tensor.matmul_mx(
                out=bank[:], lhsT=codes[:, at - begin : at - begin + P].bitcast(FP8X4), lhsT_scale=scales[:, at - begin : at - begin + P],
                rhs=whq[2][0][:].bitcast(FP8X4), rhs_scale=whq[2][1][:], start=False, stop=True,
            )
            gelus = place([P, 4, P], F32, f"gelus{block}", TURNED_AT + 2 * KB * block)
            nc.scalar.activation(gelus[:], bank[:].rearrange("j (p t) -> j t p", t=4), GELU)
            return gelus

        def dealt_tile(i):
            t = i - 4
            acts[i, 0] = place([P, S], F32, f"act{i}", ACT_AT + 4 * KB * t)
            for h in range(2):
                bank = banks[2 * (t % 2) + h]
                for b in range(4):
                    nc.tensor.transpose(bank[:, P * b : P * (b + 1)], turned_gelus[4 * h + b][:, t, :], identity[:])
                nc.scalar.activation(acts[i, 0][:, N * h : N * (h + 1)], bank[:], COPY, scale=dealt_gains[:, t : t + 1])

        def round_into_pairs(i, c):
            t = i - 4
            nc.scalar.copy(pairs[c][:, t // 2, :, t % 2], pages[i][:, N * c : N * (c + 1)])

        def weave(copy, c):
            grouped = place([P, 4 * N], BF16, f"page_g1{c}", TURNED_AT + 4 * KB * c)
            copy(
                grouped[:].bitcast(F32).rearrange("p (c u) -> p c u", u=2),
                pairs[c][:].rearrange("p u c e -> p u (c e)").bitcast(F32).rearrange("p u c -> p c u"),
            )
            return grouped

        gather_v(0, N, S)
        hand_g0 = group_hand(0)
        turn_gains(0, 2, banks[0])
        whq = [quantize(group(wh_raw[0], "wh_g0", GROUPED_AT + 8 * KB, nc.vector.tensor_copy), "wh0")]
        handq = {(0, N): quantize(hand_g0, "hand0")}
        for lo, hi in ((0, QUARTER), (QUARTER, N), (N, S)):
            gather_v(1, lo, hi)
        make_weights(0, 0, N, HAND_AT + 4 * KB)
        acts[0, 0] = place([P, N], F32, "act0_0", ACT_AT)
        for lo in (0, QUARTER):
            first_product(0, lo, lo + QUARTER, acts[0, 0][:, lo : lo + QUARTER])
        make_weights(1, 0, N, HAND_AT + 6 * KB)
        part_tile(1, 0, N, ACT_AT + 4 * KB)
        hand_g2 = group_hand(2)
        scatter(0, 0, N)
        handq[512, 768] = quantize(hand_g2, "hand2")
        scatter(1, 0, N)
        handq[768, S] = quantize(group_hand(3), "hand3")
        make_weights(0, 512, 768, HAND_AT + 12 * KB)
        part_tile(0, 512, 768, HAND_AT + 13 * KB)
        turn_gains(2, 4, banks[7])
        wh_g1 = group_wh(1, GROUPED_AT + 6 * KB)
        make_weights(0, 768, S, HAND_AT + 14 * KB)
        part_tile(0, 768, S, ACT_AT + 2 * KB)
        make_weights(1, N, S, HAND_AT + 15 * KB)
        part_tile(1, N, S, ACT_AT + 6 * KB)
        scatter(0, 512, 768)
        whq.append(quantize(wh_g1, "wh1"))
        scatter(0, 768, S)
        wh_g2 = group_wh(2, GROUPED_AT + 12 * KB)
        scatter(1, N, S)
        whq.append(quantize(wh_g2, "wh2"))
        for i in (2, 3):
            whole_tile(i)
        turned_gelus = [turned_product(block) for block in range(8)]

        for i in range(4):
            if i >= 1:
                scatter(i + 1, 0, S)
            dealt_tile(i + 4)
            for c in range(4):
                turn_and_round(i, c, banks[2 * (i % 2) + c % 2])
            if i in (1, 2):
                load_dealt_wgs(i + 5)
                pages.append(load_page(i + 5))
        tab2 = [load_table_words(tab2_words, a, f"tab2_{a}") for a in range(2)]
        cap_rows = place([P, 4, S], F32, "cap_rows", WH_AT)
        nc.sync.dma_start(cap_rows[:], cap.rearrange("(n p) m -> p n m", n=4))
        woven = [turn_back(c) for c in range(4)]
        pairs = [place([P, 2, N, 2], BF16, f"pairs{c}", HAND_AT + 4 * KB * c) for c in range(4)]
        for i in range(4, 7):
            scatter(i + 1, 0, S)
            for c in range(4):
                round_into_pairs(i, c)

        last_act = ACT_AT + 4 * KB * 3
        last_weights = WEIGHTS_AT + 4 * KB * 3
        v2_plane = place([P, S2], U8, "v2_plane", last_act + 2 * KB)
        nc.vector.tensor_copy(v2_plane[:], tab2_plane[:].indirect(idx2[:]))
        v2 = [place([P, 2, S2 // 2], U32, "v2_0", last_weights)]

        def gather_v2(u, a):
            nc.vector.tensor_copy(v2[u][:, a, :], tab2[a][:].indirect(idx2[:, 16 * u : 16 * u + 16]))

        def second_product(n, c):
            for a in range(2):
                nc.tensor.matmul_mx(
                    out=banks[4 * (n % 2) + c][:], lhsT=v2[n // 2][:, a, P * (n % 2) : P * (n % 2 + 1)].bitcast(FP8X4),
                    lhsT_scale=v2_plane[4 * a : P, P * n : P * (n + 1)],
                    rhs=pageq[a][c][0][:].bitcast(FP8X4), rhs_scale=pageq[a][c][1][:], start=(a == 0), stop=(a == 1),
                )

        for a in range(2):
            gather_v2(0, a)
        for c in range(4):
            round_into_pairs(7, c)
        last = [weave(nc.vector.tensor_copy if c == 0 else nc.scalar.copy, c) for c in range(4)]
        pageq = [[quantize(woven[c], f"page0{c}", place([P, N], U8, f"page0{c}_scales", last_act + N * c)) for c in range(4)], []]
        for c in range(4):
            pageq[1].append(quantize(last[c], f"page1{c}"))
        v2.append(place([P, 2, S2 // 2], U32, "v2_1", TURNED_AT + 12 * KB))
        for a in range(2):
            gather_v2(1, a)

        scores = [place([P, T], F32, f"scores{n}", PAGE_AT + 8 * KB * n) for n in range(4)]

        def score(n):
            for c in range(4):
                second_product(n, c)
                nc.scalar.copy(scores[n][:, c * N : (c + 1) * N], banks[4 * (n % 2) + c][:])

        def pick(n, lo, hi):
            picked = place([P, hi - lo], F32, f"picked{n}_{lo}", PAGE_AT + 8 * KB * (4 + n) if lo == 0 else ACT_AT + 4 * KB + 4 * lo)
            nc.vector.tensor_copy(picked[:], scores[n][:].indirect(idx4[:, lo // 16 : hi // 16]))
            return picked

        def cap_and_store(n, lo, hi, picked, capped):
            nc.vector.tensor_tensor(capped[:], picked[:], cap_rows[:, n, lo:hi], MIN)
            nc.sync.dma_start(out[P * n : P * (n + 1), lo:hi], capped[:])

        score(0)
        first = pick(0, 0, S)
        excess = place([P, S], F32, "excess", ACT_AT)
        nc.gpsimd.tensor_tensor(excess[:], first[:], cap_rows[:, 0, :], SUB)
        nc.gpsimd.tensor_scalar(excess[:], excess[:], float("inf"), 0.0, MIN, MAX)
        nc.gpsimd.tensor_tensor(first[:], first[:], excess[:], SUB)
        nc.sync.dma_start(out[0:P, :], first[:])
        score(1)
        second = pick(1, 0, S)
        score(2)
        third = pick(2, 0, S)
        score(3)
        cap_and_store(3, 0, N, pick(3, 0, N), place([P, N], F32, "capped3", ACT_AT))
        cap_and_store(1, 0, S, second, place([P, S], F32, "capped1", PAGE_AT + 53 * KB))
        next_to_last = pick(3, 512, 768)
        cap_and_store(2, 0, S, third, place([P, S], F32, "capped2", PAGE_AT + 57 * KB))
        very_last = pick(3, 768, S)
        cap_and_store(3, 512, 768, next_to_last, next_to_last)
        cap_and_store(3, 768, S, very_last, very_last)
